import numpy as np
import ml_dtypes


def mxq(x, axis, fmt="e4m3"):
    dtype, down = {"e4m3": (ml_dtypes.float8_e4m3fn, 7), "e5m2": (ml_dtypes.float8_e5m2, 14)}[fmt]
    v = np.moveaxis(np.asarray(x, np.float32).astype(ml_dtypes.bfloat16).astype(np.float64), axis, -1)
    blocks = v.reshape(v.shape[:-1] + (-1, 32))
    amax = np.abs(blocks).max(-1, keepdims=True)
    byte = np.maximum(np.where(amax > 0, np.frexp(amax)[1] - 1 + 127, 0) - down, 1)
    scale = np.exp2(byte - 127.0)
    codes = (blocks / scale).astype(np.float32).astype(dtype).astype(np.float64)
    return np.moveaxis((codes * scale).reshape(v.shape), -1, axis)


WIDE = False


def mx_kscale(k):
    if not WIDE:
        return np.ones(k)
    levels = np.array([10, -10, 5, -5, 0])
    if k % 512:
        return np.exp2(np.random.permutation(np.resize(levels, k // 32))).repeat(32)
    a = np.empty((k // 512, 16))
    for p in range(k // 512):
        a[p, :8] = np.random.permutation(np.resize(levels, 8))
        for g in range(8):
            far = levels[np.abs(levels - a[p, g]) >= 10]
            a[p, g + 8] = far[np.random.randint(len(far))]
    return np.exp2(a.ravel()).repeat(32)


def f64(x):
    return np.asarray(x).astype(np.float64)


def striped(idx):
    return np.tile(idx.reshape(-1, 16).T, (8, 1)).astype(np.uint16)


def unstriped(offs):
    return offs[:16].T.reshape(-1).astype(np.int64)


def gelu(v):
    return 0.5 * v * (1.0 + np.tanh(np.sqrt(2.0 / np.pi) * (v + 0.044715 * v**3)))


K, T, S, H, N = 512, 2048, 1024, 512, 256
P = 2 ** 7


def setup_inputs():
    n = np.random.standard_normal
    s = mx_kscale(K)[:, None]
    u = mx_kscale(H)
    return {
        "xT": (n((K, T)) * s).astype(np.float32),
        "w1": (n((K, H)) / np.sqrt(K) / s * u).astype(np.float32),
        "w2": (n((H, N)) / np.sqrt(H) / u[:, None]).astype(np.float32),
        "share": np.tile(np.random.uniform(0.1, 0.9, S), (P, 1)).astype(np.float32),
        "offs": striped(np.random.permutation(T)[:S]),
        "par": striped(np.random.permutation(S)[(S * np.random.uniform(0, 1, S) ** 4).astype(np.int64)]),
    }


def reference(xT, w1, w2, share, offs, par):
    xq = mxq(f64(xT)[:, unstriped(offs)], 0, "e4m3")
    h = gelu(mxq(f64(w1), 0, "e4m3").T @ xq)
    z = h + h[:, unstriped(par)] * f64(share)[:1]
    return mxq(f64(w2), 0, "e4m3").T @ mxq(z, 0, "e4m3")

@@ -1,0 +1,188 @@
+from contextlib import ExitStack
+
+import concourse.mybir as mybir
+
+K, T, S, H, N = 512, 2048, 1024, 512, 256
+FLOPS = 2 * K * H * S + 2 * H * N * S
+
+F32 = mybir.dt.float32
+BF16 = mybir.dt.bfloat16
+U32 = mybir.dt.uint32
+U16 = mybir.dt.uint16
+U8 = mybir.dt.uint8
+FP8X4 = mybir.dt.float8_e4m3fn_x4
+GELU = mybir.ActivationFunctionType.Gelu_apprx_tanh
+MULT = mybir.AluOpType.mult
+ADD = mybir.AluOpType.add
+
+P = 128
+PACK = 4
+STRIPE = 16
+
+X_LOADS = (
+    ((0, 1024, (("vector", 0, 1024),)),
+     (1024, 512, (("scalar", 0, 512),)),
+     (1536, 512, (("vector", 0, 256), ("scalar", 256, 256)))),
+    ((0, 1024, (("scalar", 0, 1024),)),
+     (1024, 512, (("vector", 0, 512),)),
+     (1536, 256, (("vector", 0, 256),)),
+     (1792, 256, (("vector", 0, 256),))),
+)
+X_PIECES = ((0, 512), (512, 256), (768, 256))
+Z_PIECES = ((0, 512), (512, 256), (768, 128), (896, 128))
+
+
+def tile_picked_treeup_gelu_e_kernel(tc, xT, w1, w2, share, offs, par, out):
+    nc = tc.nc
+
+    def copy(engine, out, in_):
+        if engine == "vector":
+            nc.vector.tensor_copy(out=out, in_=in_)
+        else:
+            nc.scalar.copy(out=out, in_=in_)
+
+    def entries(lst, first, count):
+        return lst[:, first // STRIPE : (first + count) // STRIPE]
+
+    with ExitStack() as ctx:
+        keep = ctx.enter_context(tc.tile_pool(name="keep", bufs=1))
+        ring = ctx.enter_context(tc.tile_pool(name="ring", bufs=2))
+        psum_h = ctx.enter_context(tc.psum_pool(name="psum_h", bufs=6))
+        psum_o = ctx.enter_context(tc.psum_pool(name="psum_o", bufs=2))
+
+        offs_t = keep.tile([P, S // STRIPE], U16, name="offs_t")
+        par_t = keep.tile([P, S // STRIPE], U16, name="par_t")
+
+        warm_in = keep.tile([P, 8], F32, name="warm_in")
+        warm_out = keep.tile([P, 8], F32, name="warm_out")
+        nc.vector.memset(warm_in[:], 0.0)
+        nc.scalar.activation(out=warm_out[:], in_=warm_in[:], func=GELU)
+
+        x_rows = xT.rearrange("(p j) t -> p j t", j=PACK)
+        raw = {}
+        for u in range(2):
+            for first, cols, shares in X_LOADS[u]:
+                raw[u, first] = keep.tile([P, 2, cols], F32, name="x_raw_%d_%d" % (u, first))
+                nc.sync.dma_start(out=raw[u, first][:], in_=x_rows[:, 2 * u : 2 * u + 2, first : first + cols])
+                if (u, first) == (0, 0):
+                    nc.sync.dma_start(offs_t[:], offs)
+        w1_rows = w1.rearrange("(p j) c -> p j c", j=PACK)
+        w1_raw = []
+        for half in range(2):
+            w1_raw.append(keep.tile([P, PACK, H // 2], F32, name="w1_raw_%d" % half))
+            nc.sync.dma_start(out=w1_raw[half][:], in_=w1_rows[:, :, half * (H // 2) : (half + 1) * (H // 2)])
+        share_t = keep.tile([P, S], F32, name="share_t")
+        nc.sync.dma_start(out=share_t[:], in_=share)
+        nc.sync.dma_start(par_t[:], par)
+        w2_raw = keep.tile([P, PACK, N], F32, name="w2_raw")
+        nc.sync.dma_start(out=w2_raw[:], in_=w2.rearrange("(p j) n -> p j n", j=PACK))
+
+        pairs = [keep.tile([P, T], U32, name="pairs_%d" % u) for u in range(2)]
+        x_bf = [keep.tile([P, PACK * n], BF16, name="x_bf_%d" % first, align_bytes=64) for first, n in X_PIECES]
+        x_codes = [keep.tile([P, n], U32, name="x_codes_%d" % first, align_bytes=64) for first, n in X_PIECES]
+        x_scales = [keep.tile([P, n], U8, name="x_scales_%d" % first, align_bytes=64) for first, n in X_PIECES]
+
+        def pair_up(u):
+            view = pairs[u][:].bitcast(BF16).rearrange("p (t e) -> p t e", e=2)
+            for first, cols, shares in X_LOADS[u]:
+                for engine, start, count in shares:
+                    copy(engine, view[:, first + start : first + start + count, :],
+                         raw[u, first][:, :, start : start + count].rearrange("p e t -> p t e"))
+
+        def pick(u, i):
+            first, n = X_PIECES[i]
+            words = x_bf[i][:].bitcast(U32).rearrange("p (t u) -> p t u", u=2)
+            nc.vector.tensor_copy(out=words[:, :, u], in_=pairs[u][:].indirect(entries(offs_t, first, n)))
+
+        def quantize(codes, scales, values):
+            nc.vector.quantize_mx(out=codes.bitcast(FP8X4), scales=scales, in_=values)
+
+        pair_up(0)
+        for i in range(len(X_PIECES)):
+            pick(0, i)
+        pair_up(1)
+
+        w1_bf = keep.tile([P, PACK, P, PACK], BF16, name="w1_bf", align_bytes=64)
+        for half in range(2):
+            nc.scalar.copy(
+                out=w1_bf[:, :, half * (P // 2) : (half + 1) * (P // 2), :].rearrange("p t m j -> p m j t"),
+                in_=w1_raw[half][:].rearrange("p j (m t) -> p m j t", t=PACK))
+        w1_codes = [keep.tile([P, P], U32, name="w1_codes_%d" % t, align_bytes=64) for t in range(PACK)]
+        w1_scales = [keep.tile([P, P], U8, name="w1_scales_%d" % t, align_bytes=64) for t in range(PACK)]
+
+        def quantize_w1(t):
+            quantize(w1_codes[t][:], w1_scales[t][:], w1_bf[:, t, :, :].rearrange("p m j -> p (m j)"))
+
+        pick(1, 0)
+        pick(1, 1)
+        quantize(x_codes[0][:], x_scales[0][:], x_bf[0][:])
+        quantize_w1(0)
+        pick(1, 2)
+        quantize(x_codes[1][:], x_scales[1][:], x_bf[1][:])
+        quantize(x_codes[2][:], x_scales[2][:], x_bf[2][:])
+        for t in range(1, PACK):
+            quantize_w1(t)
+
+        w2_bf = keep.tile([P, N, PACK], BF16, name="w2_bf", align_bytes=64)
+        nc.scalar.copy(out=w2_bf[:].rearrange("p (c i) j -> p c j i", i=4),
+                       in_=w2_raw[:].rearrange("p j (c i) -> p c j i", i=4))
+        w2_codes = keep.tile([P, N], U32, name="w2_codes", align_bytes=64)
+        w2_scales = keep.tile([P, N], U8, name="w2_scales", align_bytes=64)
+
+        h = [keep.tile([P, S], F32, name="h_%d" % t) for t in range(PACK)]
+        for t in range(PACK):
+            for i, (first, n) in enumerate(X_PIECES):
+                acc = psum_h.tile([P, 512], F32, name="acc_h")
+                nc.tensor.matmul_mx(out=acc[:, 0:n], lhsT=w1_codes[t][:].bitcast(FP8X4), lhsT_scale=w1_scales[t][:],
+                                    rhs=x_codes[i][:].bitcast(FP8X4), rhs_scale=x_scales[i][:], start=True, stop=True)
+                nc.scalar.activation(out=h[t][:, first : first + n], in_=acc[:, 0:n], func=GELU)
+
+        quantize(w2_codes[:], w2_scales[:], w2_bf[:].rearrange("p n j -> p (n j)"))
+
+        out_rows = out.rearrange("(a p) j -> p a j", p=P)
+        taken, z_planes, z_bf = {}, {}, {}
+
+        def take(i, t):
+            first, n = Z_PIECES[i]
+            taken[i, t] = ring.tile([P, n], F32, name="taken")
+            nc.vector.tensor_tensor(out=taken[i, t][:], in0=h[t][:].indirect(entries(par_t, first, n)),
+                                    in1=share_t[:, first : first + n], op=MULT)
+
+        def add(i, t):
+            first, n = Z_PIECES[i]
+            if t == 0:
+                z_planes[i] = ring.tile([P, PACK, n], BF16, name="z_planes")
+            nc.vector.tensor_tensor(out=z_planes[i][:, t, :], in0=taken[i, t][:], in1=h[t][:, first : first + n], op=ADD)
+            if t == PACK - 1:
+                z_bf[i] = keep.tile([P, n, PACK], BF16, name="z_bf_%d" % i, align_bytes=64)
+                nc.scalar.copy(out=z_bf[i][:].rearrange("p (c i) t -> p c t i", i=4),
+                               in_=z_planes[i][:].rearrange("p t (c i) -> p c t i", i=4))
+
+        def finish(i):
+            first, n = Z_PIECES[i]
+            codes = keep.tile([P, n], U32, name="z_codes_%d" % i, align_bytes=64)
+            scales = keep.tile([P, n], U8, name="z_scales_%d" % i, align_bytes=64)
+            quantize(codes[:], scales[:], z_bf[i][:].rearrange("p n t -> p (n t)"))
+            result = keep.tile([P, N // P, n], F32, name="result_%d" % i)
+            per_bank = min(N // P, 512 // n)
+            for a0 in range(0, N // P, per_bank):
+                acc = psum_o.tile([P, 512], F32, name="acc_o")
+                for a in range(a0, a0 + per_bank):
+                    nc.tensor.matmul_mx(out=acc[:, (a - a0) * n : (a - a0 + 1) * n],
+                                        lhsT=w2_codes[:, a * P : (a + 1) * P].bitcast(FP8X4),
+                                        lhsT_scale=w2_scales[:, a * P : (a + 1) * P],
+                                        rhs=codes[:].bitcast(FP8X4), rhs_scale=scales[:], start=True, stop=True)
+                nc.scalar.copy(out=result[:, a0 : a0 + per_bank, :].rearrange("p a n -> p (a n)"),
+                               in_=acc[:, 0 : per_bank * n])
+            nc.sync.dma_start(out=out_rows[:, :, first : first + n], in_=result[:])
+
+        steps = [(i, t) for i in range(len(Z_PIECES)) for t in range(PACK)]
+        for s, (i, t) in enumerate(steps):
+            take(i, t)
+            if s >= 1:
+                add(*steps[s - 1])
+            if i >= 2 and t == 0:
+                finish(i - 2)
+        add(*steps[-1])
+        finish(len(Z_PIECES) - 2)
+        finish(len(Z_PIECES) - 1)

@@ -1,6 +1,7 @@
 from contextlib import ExitStack
 
 import concourse.mybir as mybir
+from concourse.masks import make_identity
 
 K, T, S, H, N = 512, 2048, 1024, 512, 256
 FLOPS = 2 * K * H * S + 2 * H * N * S
@@ -28,8 +29,12 @@ X_LOADS = (
      (1536, 256, (("vector", 0, 256),)),
      (1792, 256, (("vector", 0, 256),))),
 )
-X_PIECES = ((0, 512), (512, 256), (768, 256))
-Z_PIECES = ((0, 512), (512, 256), (768, 128), (896, 128))
+X_PIECES = ((0, 512), (512, 512))
+Z_PIECES = ((0, 256), (256, 256), (512, 256), (768, 128), (896, 128))
+BANK = 512
+SUM_BANKS = (0, 2, 6, 5)
+BACK_BANKS = (4, 5, 2, 4)
+OUT_BANKS = (0, 1, 3, 6, 0)
 
 
 def tile_picked_treeup_gelu_e_kernel(tc, xT, w1, w2, share, offs, par, out):
@@ -47,8 +52,12 @@ def tile_picked_treeup_gelu_e_kernel(tc, xT, w1, w2, share, offs, par, out):
     with ExitStack() as ctx:
         keep = ctx.enter_context(tc.tile_pool(name="keep", bufs=1))
         ring = ctx.enter_context(tc.tile_pool(name="ring", bufs=2))
-        psum_h = ctx.enter_context(tc.psum_pool(name="psum_h", bufs=6))
-        psum_o = ctx.enter_context(tc.psum_pool(name="psum_o", bufs=2))
+        single = ctx.enter_context(tc.tile_pool(name="single", bufs=1))
+        psum = ctx.enter_context(tc.psum_pool(name="psum", bufs=1))
+
+        def bank(number):
+            return psum.tile([P, BANK], F32, name="bank_%d" % number)
+
 
         offs_t = keep.tile([P, S // STRIPE], U16, name="offs_t")
         par_t = keep.tile([P, S // STRIPE], U16, name="par_t")
@@ -57,6 +66,9 @@ def tile_picked_treeup_gelu_e_kernel(tc, xT, w1, w2, share, offs, par, out):
         warm_out = keep.tile([P, 8], F32, name="warm_out")
         nc.vector.memset(warm_in[:], 0.0)
         nc.scalar.activation(out=warm_out[:], in_=warm_in[:], func=GELU)
+
+        ident = keep.tile([P, P], F32, name="ident")
+        make_identity(nc, ident[:])
 
         x_rows = xT.rearrange("(p j) t -> p j t", j=PACK)
         raw = {}
@@ -116,11 +128,8 @@ def tile_picked_treeup_gelu_e_kernel(tc, xT, w1, w2, share, offs, par, out):
         pick(1, 0)
         pick(1, 1)
         quantize(x_codes[0][:], x_scales[0][:], x_bf[0][:])
-        quantize_w1(0)
-        pick(1, 2)
         quantize(x_codes[1][:], x_scales[1][:], x_bf[1][:])
-        quantize(x_codes[2][:], x_scales[2][:], x_bf[2][:])
-        for t in range(1, PACK):
+        for t in range(PACK):
             quantize_w1(t)
 
         w2_bf = keep.tile([P, N, PACK], BF16, name="w2_bf", align_bytes=64)
@@ -132,7 +141,7 @@ def tile_picked_treeup_gelu_e_kernel(tc, xT, w1, w2, share, offs, par, out):
         h = [keep.tile([P, S], F32, name="h_%d" % t) for t in range(PACK)]
         for t in range(PACK):
             for i, (first, n) in enumerate(X_PIECES):
-                acc = psum_h.tile([P, 512], F32, name="acc_h")
+                acc = bank(2 * t + i)
                 nc.tensor.matmul_mx(out=acc[:, 0:n], lhsT=w1_codes[t][:].bitcast(FP8X4), lhsT_scale=w1_scales[t][:],
                                     rhs=x_codes[i][:].bitcast(FP8X4), rhs_scale=x_scales[i][:], start=True, stop=True)
                 nc.scalar.activation(out=h[t][:, first : first + n], in_=acc[:, 0:n], func=GELU)
@@ -140,49 +149,94 @@ def tile_picked_treeup_gelu_e_kernel(tc, xT, w1, w2, share, offs, par, out):
         quantize(w2_codes[:], w2_scales[:], w2_bf[:].rearrange("p n j -> p (n j)"))
 
         out_rows = out.rearrange("(a p) j -> p a j", p=P)
-        taken, z_planes, z_bf = {}, {}, {}
+        z_bf, sums = {}, {}
 
         def take(i, t):
             first, n = Z_PIECES[i]
-            taken[i, t] = ring.tile([P, n], F32, name="taken")
-            nc.vector.tensor_tensor(out=taken[i, t][:], in0=h[t][:].indirect(entries(par_t, first, n)),
+            blocks = n // P
+            taken = ring.tile([P, n], F32, name="taken")
+            nc.vector.tensor_tensor(out=taken[:], in0=h[t][:].indirect(entries(par_t, first, n)),
                                     in1=share_t[:, first : first + n], op=MULT)
+            return taken
 
-        def add(i, t):
+        def sum_on_vector(i):
             first, n = Z_PIECES[i]
+            blocks = n // P
+            planes = single.tile([P, PACK, n], BF16, name="z_planes")
+            taken = [take(i, 0)]
+            for t in range(PACK):
+                if t + 1 < PACK:
+                    taken.append(take(i, t + 1))
+                nc.vector.tensor_tensor(out=planes[:, t, :], in0=taken[t][:], in1=h[t][:, first : first + n], op=ADD)
+            z_bf[i] = single.tile([P, PACK * n], BF16, name="z_bf_%d" % (i - 1), align_bytes=64)
+            for engine, lo, hi in (("scalar", 0, 48), ("vector", 48, n)):
+                copy(engine, z_bf[i][:, PACK * lo : PACK * hi].rearrange("p (c i t) -> p c t i", i=4, t=PACK),
+                     planes[:, :, lo:hi].rearrange("p t (c i) -> p c t i", i=4))
+
+        def plane_on_tensor(i, t):
+            first, n = Z_PIECES[i]
+            blocks = n // P
             if t == 0:
-                z_planes[i] = ring.tile([P, PACK, n], BF16, name="z_planes")
-            nc.vector.tensor_tensor(out=z_planes[i][:, t, :], in0=taken[i, t][:], in1=h[t][:, first : first + n], op=ADD)
-            if t == PACK - 1:
-                z_bf[i] = keep.tile([P, n, PACK], BF16, name="z_bf_%d" % i, align_bytes=64)
-                nc.scalar.copy(out=z_bf[i][:].rearrange("p (c i) t -> p c t i", i=4),
-                               in_=z_planes[i][:].rearrange("p t (c i) -> p c t i", i=4))
+                sums[i] = [bank(SUM_BANKS[i] + b) for b in range(blocks)]
+            for b in range(blocks):
+                nc.tensor.matmul(out=sums[i][b][:, t * P : (t + 1) * P], lhsT=h[t][:, first + b * P : first + (b + 1) * P],
+                                 rhs=ident[:], start=True, stop=False, is_transpose=True)
+            taken = take(i, t)
+            for b in range(blocks):
+                nc.tensor.matmul(out=sums[i][b][:, t * P : (t + 1) * P], lhsT=taken[:, b * P : (b + 1) * P],
+                                 rhs=ident[:], start=False, stop=True, is_transpose=True)
 
-        def finish(i):
+        def turn_back(i):
             first, n = Z_PIECES[i]
+            blocks = n // P
+            z_rows = ring.tile([P, blocks * H], BF16, name="z_rows")
+            z_bf[i] = single.tile([P, PACK * n], BF16, name="z_bf_%d" % i, align_bytes=64)
+            back = bank(BACK_BANKS[i])
+            for b in range(blocks):
+                nc.scalar.copy(out=z_rows[:, b * H : (b + 1) * H].rearrange("r (u p e) -> r u p e", u=2, e=2),
+                               in_=sums[i][b][:].rearrange("r (u e p) -> r u p e", u=2, e=2))
+                words = z_rows[:, b * H : (b + 1) * H].bitcast(F32)
+                for u in range(2):
+                    col = (b * 2 + u) * P
+                    nc.tensor.transpose(back[:, col : col + P], words[:, u * P : (u + 1) * P], ident[:])
+            nc.scalar.copy(out=z_bf[i][:].bitcast(F32).rearrange("p (b r u) -> p b r u", b=blocks, u=2),
+                           in_=back[:, 0 : 2 * n].rearrange("p (b u r) -> p b r u", b=blocks, u=2))
+
+        def finish(i, last):
+            first, n = Z_PIECES[i]
+            blocks = n // P
             codes = keep.tile([P, n], U32, name="z_codes_%d" % i, align_bytes=64)
             scales = keep.tile([P, n], U8, name="z_scales_%d" % i, align_bytes=64)
-            quantize(codes[:], scales[:], z_bf[i][:].rearrange("p n t -> p (n t)"))
+            quantize(codes[:], scales[:], z_bf[i][:])
             result = keep.tile([P, N // P, n], F32, name="result_%d" % i)
-            per_bank = min(N // P, 512 // n)
-            for a0 in range(0, N // P, per_bank):
-                acc = psum_o.tile([P, 512], F32, name="acc_o")
-                for a in range(a0, a0 + per_bank):
-                    nc.tensor.matmul_mx(out=acc[:, (a - a0) * n : (a - a0 + 1) * n],
-                                        lhsT=w2_codes[:, a * P : (a + 1) * P].bitcast(FP8X4),
-                                        lhsT_scale=w2_scales[:, a * P : (a + 1) * P],
-                                        rhs=codes[:].bitcast(FP8X4), rhs_scale=scales[:], start=True, stop=True)
-                nc.scalar.copy(out=result[:, a0 : a0 + per_bank, :].rearrange("p a n -> p (a n)"),
-                               in_=acc[:, 0 : per_bank * n])
+            acc = bank(OUT_BANKS[i])
+            for a in range(N // P):
+                if last and a == 1:
+                    acc = bank(OUT_BANKS[i] + 1)
+                nc.tensor.matmul_mx(out=acc[:, a * n : (a + 1) * n],
+                                    lhsT=w2_codes[:, a * P : (a + 1) * P].bitcast(FP8X4),
+                                    lhsT_scale=w2_scales[:, a * P : (a + 1) * P],
+                                    rhs=codes[:].bitcast(FP8X4), rhs_scale=scales[:], start=True, stop=True)
+                if last:
+                    copy(("scalar", "vector")[a], result[:, a, :], acc[:, a * n : (a + 1) * n])
+            if not last:
+                nc.scalar.copy(out=result[:].rearrange("p a n -> p (a n)"), in_=acc[:, 0 : 2 * n])
             nc.sync.dma_start(out=out_rows[:, :, first : first + n], in_=result[:])
 
-        steps = [(i, t) for i in range(len(Z_PIECES)) for t in range(PACK)]
-        for s, (i, t) in enumerate(steps):
-            take(i, t)
-            if s >= 1:
-                add(*steps[s - 1])
-            if i >= 2 and t == 0:
-                finish(i - 2)
-        add(*steps[-1])
-        finish(len(Z_PIECES) - 2)
-        finish(len(Z_PIECES) - 1)
+        for t in range(PACK):
+            plane_on_tensor(0, t)
+            plane_on_tensor(1, t)
+        turn_back(0)
+        turn_back(1)
+        finish(0, False)
+        for t in range(PACK):
+            plane_on_tensor(2, t)
+        finish(1, False)
+        turn_back(2)
+        for t in range(PACK):
+            plane_on_tensor(3, t)
+        finish(2, False)
+        turn_back(3)
+        finish(3, False)
+        sum_on_vector(4)
+        finish(4, True)

@@ -19,22 +19,27 @@ ADD = mybir.AluOpType.add
 P = 128
 PACK = 4
 STRIPE = 16
+BANK = 512
 
 X_LOADS = (
     ((0, 1024, (("vector", 0, 1024),)),
-     (1024, 512, (("scalar", 0, 512),)),
-     (1536, 512, (("vector", 0, 256), ("scalar", 256, 256)))),
-    ((0, 1024, (("scalar", 0, 1024),)),
      (1024, 512, (("vector", 0, 512),)),
+     (1536, 512, (("vector", 0, 320), ("scalar", 320, 192)))),
+    ((0, 512, (("scalar", 0, 512),)),
+     (512, 512, (("scalar", 0, 512),)),
+     (1024, 512, (("vector", 0, 256), ("scalar", 256, 256))),
      (1536, 256, (("vector", 0, 256),)),
      (1792, 256, (("vector", 0, 256),))),
 )
-X_PIECES = ((0, 512), (512, 512))
+X_PIECES = ((0, 256, "vector"), (256, 256, "vector"), (512, 256, "scalar"), (768, 256, "scalar"))
+Q_PIECES = ((0, 256), (256, 256), (512, 256), (768, 256))
+EARLY = 1
+H_BANKS = (((0, (0,)), (1, (1,)), (2, (2,)), (3, (3,))), ((4, (0, 1)), (5, (2, 3))), ((6, (0, 1)), (7, (2, 3))), ((0, (0, 1)), (1, (2, 3))))
 Z_PIECES = ((0, 256), (256, 256), (512, 256), (768, 128), (896, 128))
-BANK = 512
-SUM_BANKS = (0, 2, 6, 5)
-BACK_BANKS = (4, 5, 2, 4)
-OUT_BANKS = (0, 1, 3, 6, 0)
+SUM_BANKS = {0: 2, 1: 4, 2: 6}
+BACK_BANKS = {0: 0, 1: 1, 2: 2}
+OUT_BANKS = (3, 4, 5, 0, 1)
+AFTER = {"taken_2_2": "taken_0_3", "taken_2_1": "taken_1_3", "taken_2_0": "taken_2_3", "taken_3_3": "taken_2_2", "taken_3_2": "taken_2_1", "taken_3_1": "taken_2_0", "taken_3_0": "taken_3_3", "taken_4_3": "taken_3_2", "taken_4_2": "taken_3_1", "taken_4_1": "taken_3_0", "taken_4_0": "taken_4_3", "x_scales_late": "w1_bf_0", "w2_bf": "x_codes_3", "z_planes_3": "z_bf_0", "z_planes_4": "z_bf_1", "z_codes_4": "z_bf_2"}
 
 
 def tile_picked_treeup_gelu_e_kernel(tc, xT, w1, w2, share, offs, par, out):
@@ -49,50 +54,54 @@ def tile_picked_treeup_gelu_e_kernel(tc, xT, w1, w2, share, offs, par, out):
     def entries(lst, first, count):
         return lst[:, first // STRIPE : (first + count) // STRIPE]
 
+    def quantize(codes, scales, values):
+        nc.vector.quantize_mx(out=codes.bitcast(FP8X4), scales=scales, in_=values)
+
     with ExitStack() as ctx:
+        lists = ctx.enter_context(tc.tile_pool(name="lists", bufs=1))
         keep = ctx.enter_context(tc.tile_pool(name="keep", bufs=1))
-        ring = ctx.enter_context(tc.tile_pool(name="ring", bufs=2))
-        single = ctx.enter_context(tc.tile_pool(name="single", bufs=1))
         psum = ctx.enter_context(tc.psum_pool(name="psum", bufs=1))
+
+        def tile(name, shape, dtype):
+            while name in AFTER:
+                name = AFTER[name]
+            return keep.tile(shape, dtype, name=name, align_bytes=64)
 
         def bank(number):
             return psum.tile([P, BANK], F32, name="bank_%d" % number)
 
+        offs_t = lists.tile([P, S // STRIPE], U16, name="offs_t")
+        par_t = lists.tile([P, S // STRIPE], U16, name="par_t")
 
-        offs_t = keep.tile([P, S // STRIPE], U16, name="offs_t")
-        par_t = keep.tile([P, S // STRIPE], U16, name="par_t")
-
-        warm_in = keep.tile([P, 8], F32, name="warm_in")
-        warm_out = keep.tile([P, 8], F32, name="warm_out")
+        warm_in = tile("warm_in", [P, 8], F32)
+        warm_out = tile("warm_out", [P, 8], F32)
         nc.vector.memset(warm_in[:], 0.0)
         nc.scalar.activation(out=warm_out[:], in_=warm_in[:], func=GELU)
 
-        ident = keep.tile([P, P], F32, name="ident")
+        ident = tile("ident", [P, P], F32)
         make_identity(nc, ident[:])
 
         x_rows = xT.rearrange("(p j) t -> p j t", j=PACK)
         raw = {}
         for u in range(2):
             for first, cols, shares in X_LOADS[u]:
-                raw[u, first] = keep.tile([P, 2, cols], F32, name="x_raw_%d_%d" % (u, first))
+                raw[u, first] = tile("x_raw_%d_%d" % (u, first), [P, 2, cols], F32)
                 nc.sync.dma_start(out=raw[u, first][:], in_=x_rows[:, 2 * u : 2 * u + 2, first : first + cols])
                 if (u, first) == (0, 0):
                     nc.sync.dma_start(offs_t[:], offs)
         w1_rows = w1.rearrange("(p j) c -> p j c", j=PACK)
         w1_raw = []
         for half in range(2):
-            w1_raw.append(keep.tile([P, PACK, H // 2], F32, name="w1_raw_%d" % half))
+            w1_raw.append(tile("w1_raw_%d" % half, [P, PACK, H // 2], F32))
             nc.sync.dma_start(out=w1_raw[half][:], in_=w1_rows[:, :, half * (H // 2) : (half + 1) * (H // 2)])
-        share_t = keep.tile([P, S], F32, name="share_t")
+        share_t = tile("share_t", [P, S], F32)
         nc.sync.dma_start(out=share_t[:], in_=share)
         nc.sync.dma_start(par_t[:], par)
-        w2_raw = keep.tile([P, PACK, N], F32, name="w2_raw")
+        w2_raw = tile("w2_raw", [P, PACK, N], F32)
         nc.sync.dma_start(out=w2_raw[:], in_=w2.rearrange("(p j) n -> p j n", j=PACK))
 
-        pairs = [keep.tile([P, T], U32, name="pairs_%d" % u) for u in range(2)]
-        x_bf = [keep.tile([P, PACK * n], BF16, name="x_bf_%d" % first, align_bytes=64) for first, n in X_PIECES]
-        x_codes = [keep.tile([P, n], U32, name="x_codes_%d" % first, align_bytes=64) for first, n in X_PIECES]
-        x_scales = [keep.tile([P, n], U8, name="x_scales_%d" % first, align_bytes=64) for first, n in X_PIECES]
+        pairs = [tile("pairs_%d" % u, [P, T], U32) for u in range(2)]
+        x_bf, x_flat, x_codes, x_scales = {}, {}, {}, {}
 
         def pair_up(u):
             view = pairs[u][:].bitcast(BF16).rearrange("p (t e) -> p t e", e=2)
@@ -102,95 +111,137 @@ def tile_picked_treeup_gelu_e_kernel(tc, xT, w1, w2, share, offs, par, out):
                          raw[u, first][:, :, start : start + count].rearrange("p e t -> p t e"))
 
         def pick(u, i):
-            first, n = X_PIECES[i]
-            words = x_bf[i][:].bitcast(U32).rearrange("p (t u) -> p t u", u=2)
-            nc.vector.tensor_copy(out=words[:, :, u], in_=pairs[u][:].indirect(entries(offs_t, first, n)))
+            first, n, weaver = X_PIECES[i]
+            if weaver is None:
+                if u == 0:
+                    x_bf[i] = tile("x_bf_%d" % i, [P, PACK * n], BF16)
+                words = x_bf[i][:].bitcast(U32).rearrange("p (t u) -> p t u", u=2)
+                nc.vector.tensor_copy(out=words[:, :, u], in_=pairs[u][:].indirect(entries(offs_t, first, n)))
+            else:
+                if u == 0:
+                    x_flat[i] = tile("x_flat_%d" % i, [P, 2 * n], U32)
+                nc.vector.tensor_copy(out=x_flat[i][:, u * n : (u + 1) * n], in_=pairs[u][:].indirect(entries(offs_t, first, n)))
 
-        def quantize(codes, scales, values):
-            nc.vector.quantize_mx(out=codes.bitcast(FP8X4), scales=scales, in_=values)
+        def weave_x(i):
+            first, n, weaver = X_PIECES[i]
+            x_bf[i] = tile("x_bf_%d" % i, [P, PACK * n], BF16)
+            dt = U32 if weaver == "scalar" else mybir.dt.int32
+            copy(weaver, x_bf[i][:].bitcast(dt).rearrange("p (t u) -> p t u", u=2),
+                 x_flat[i][:].bitcast(dt).rearrange("p (u t) -> p t u", u=2))
+
+        late = {}
+
+        def quantize_x(q):
+            first, n = Q_PIECES[q]
+            i = [i for i, piece in enumerate(X_PIECES) if piece[0] <= first][-1]
+            x_codes[q] = tile("x_codes_%d" % q, [P, n], U32)[:]
+            if q < EARLY:
+                x_scales[q] = tile("x_scales_%d" % q, [P, n], U8)[:]
+            else:
+                if not late:
+                    late[0] = tile("x_scales_late", [P, S], U8)
+                x_scales[q] = late[0][:, first : first + n]
+            lo = first - X_PIECES[i][0]
+            quantize(x_codes[q], x_scales[q], x_bf[i][:, PACK * lo : PACK * (lo + n)])
+
+        w1_bf = [tile("w1_bf_%d" % v, [P, 2, P, PACK], BF16) for v in range(2)]
+        w1_codes, w1_scales = {}, {}
+
+        def weave_w1(half, v, engine):
+            copy(engine, w1_bf[v][:, :, half * (P // 2) : (half + 1) * (P // 2), :].rearrange("p t m j -> p m j t"),
+                 w1_raw[half][:].rearrange("p j (m t) -> p m j t", t=PACK)[:, :, :, 2 * v : 2 * v + 2])
+
+        def quantize_w1(v):
+            w1_codes[v] = tile("w1_codes_%d" % v, [P, 2 * P], U32)
+            w1_scales[v] = tile("w1_scales_%d" % v, [P, 2 * P], U8)
+            quantize(w1_codes[v][:], w1_scales[v][:], w1_bf[v][:].rearrange("p t m j -> p (t m j)"))
 
         pair_up(0)
         for i in range(len(X_PIECES)):
             pick(0, i)
         pair_up(1)
+        for i in range(len(X_PIECES)):
+            pick(1, i)
+        weave_x(0)
+        weave_x(1)
+        weave_w1(0, 0, "scalar")
+        weave_w1(0, 1, "scalar")
+        weave_w1(1, 0, "scalar")
+        weave_x(2)
+        weave_x(3)
+        weave_w1(1, 1, "scalar")
+        quantize_x(0)
+        quantize_w1(0)
+        for q in (1, 2, 3):
+            quantize_x(q)
+        quantize_w1(1)
 
-        w1_bf = keep.tile([P, PACK, P, PACK], BF16, name="w1_bf", align_bytes=64)
-        for half in range(2):
-            nc.scalar.copy(
-                out=w1_bf[:, :, half * (P // 2) : (half + 1) * (P // 2), :].rearrange("p t m j -> p m j t"),
-                in_=w1_raw[half][:].rearrange("p j (m t) -> p m j t", t=PACK))
-        w1_codes = [keep.tile([P, P], U32, name="w1_codes_%d" % t, align_bytes=64) for t in range(PACK)]
-        w1_scales = [keep.tile([P, P], U8, name="w1_scales_%d" % t, align_bytes=64) for t in range(PACK)]
-
-        def quantize_w1(t):
-            quantize(w1_codes[t][:], w1_scales[t][:], w1_bf[:, t, :, :].rearrange("p m j -> p (m j)"))
-
-        pick(1, 0)
-        pick(1, 1)
-        quantize(x_codes[0][:], x_scales[0][:], x_bf[0][:])
-        quantize(x_codes[1][:], x_scales[1][:], x_bf[1][:])
+        h = [tile("h_%d" % t, [P, S], F32) for t in range(PACK)]
         for t in range(PACK):
-            quantize_w1(t)
+            for number, members in H_BANKS[t]:
+                acc = bank(number)
+                start = Q_PIECES[members[0]][0]
+                for i in members:
+                    first, n = Q_PIECES[i]
+                    nc.tensor.matmul_mx(out=acc[:, first - start : first - start + n],
+                                        lhsT=w1_codes[t // 2][:, (t % 2) * P : (t % 2 + 1) * P].bitcast(FP8X4),
+                                        lhsT_scale=w1_scales[t // 2][:, (t % 2) * P : (t % 2 + 1) * P],
+                                        rhs=x_codes[i].bitcast(FP8X4), rhs_scale=x_scales[i], start=True, stop=True)
+                nc.scalar.activation(out=h[t][:, start : first + n], in_=acc[:, 0 : first + n - start], func=GELU)
 
-        w2_bf = keep.tile([P, N, PACK], BF16, name="w2_bf", align_bytes=64)
-        nc.scalar.copy(out=w2_bf[:].rearrange("p (c i) j -> p c j i", i=4),
-                       in_=w2_raw[:].rearrange("p j (c i) -> p c j i", i=4))
-        w2_codes = keep.tile([P, N], U32, name="w2_codes", align_bytes=64)
-        w2_scales = keep.tile([P, N], U8, name="w2_scales", align_bytes=64)
-
-        h = [keep.tile([P, S], F32, name="h_%d" % t) for t in range(PACK)]
-        for t in range(PACK):
-            for i, (first, n) in enumerate(X_PIECES):
-                acc = bank(2 * t + i)
-                nc.tensor.matmul_mx(out=acc[:, 0:n], lhsT=w1_codes[t][:].bitcast(FP8X4), lhsT_scale=w1_scales[t][:],
-                                    rhs=x_codes[i][:].bitcast(FP8X4), rhs_scale=x_scales[i][:], start=True, stop=True)
-                nc.scalar.activation(out=h[t][:, first : first + n], in_=acc[:, 0:n], func=GELU)
+        w2_bf = tile("w2_bf", [P, N, PACK], BF16)
+        copy("scalar", w2_bf[:].rearrange("p (c i) j -> p c j i", i=4), w2_raw[:].rearrange("p j (c i) -> p c j i", i=4))
+        w2_codes = tile("w2_codes", [P, N], U32)
+        w2_scales = tile("w2_scales", [P, N], U8)
 
         quantize(w2_codes[:], w2_scales[:], w2_bf[:].rearrange("p n j -> p (n j)"))
 
         out_rows = out.rearrange("(a p) j -> p a j", p=P)
-        z_bf, sums = {}, {}
+        z_bf, sums, planes, taken = {}, {}, {}, {}
 
         def take(i, t):
             first, n = Z_PIECES[i]
-            blocks = n // P
-            taken = ring.tile([P, n], F32, name="taken")
-            nc.vector.tensor_tensor(out=taken[:], in0=h[t][:].indirect(entries(par_t, first, n)),
+            taken[i, t] = tile("taken_%d_%d" % (i, t), [P, n], F32)
+            nc.vector.tensor_tensor(out=taken[i, t][:], in0=h[t][:].indirect(entries(par_t, first, n)),
                                     in1=share_t[:, first : first + n], op=MULT)
-            return taken
 
-        def sum_on_vector(i):
+        def add(i, t):
             first, n = Z_PIECES[i]
-            blocks = n // P
-            planes = single.tile([P, PACK, n], BF16, name="z_planes")
-            taken = [take(i, 0)]
-            for t in range(PACK):
-                if t + 1 < PACK:
-                    taken.append(take(i, t + 1))
-                nc.vector.tensor_tensor(out=planes[:, t, :], in0=taken[t][:], in1=h[t][:, first : first + n], op=ADD)
-            z_bf[i] = single.tile([P, PACK * n], BF16, name="z_bf_%d" % (i - 1), align_bytes=64)
-            for engine, lo, hi in (("scalar", 0, 48), ("vector", 48, n)):
-                copy(engine, z_bf[i][:, PACK * lo : PACK * hi].rearrange("p (c i t) -> p c t i", i=4, t=PACK),
-                     planes[:, :, lo:hi].rearrange("p t (c i) -> p c t i", i=4))
+            if i not in planes:
+                planes[i] = tile("z_planes_%d" % i, [P, PACK, n], BF16)
+            nc.vector.tensor_tensor(out=planes[i][:, t, :], in0=taken[i, t][:], in1=h[t][:, first : first + n], op=ADD)
+
+        def weave_z(i, engine):
+            first, n = Z_PIECES[i]
+            z_bf[i] = tile("z_bf_%d" % i, [P, PACK * n], BF16)
+            copy(engine, z_bf[i][:].rearrange("p (c i t) -> p c t i", i=4, t=PACK),
+                 planes[i][:].rearrange("p t (c i) -> p c t i", i=4))
+
+        def sum_on_vector(i, order):
+            take(i, order[0])
+            for s, t in enumerate(order):
+                if s + 1 < PACK:
+                    take(i, order[s + 1])
+                add(i, t)
 
         def plane_on_tensor(i, t):
             first, n = Z_PIECES[i]
             blocks = n // P
-            if t == 0:
+            if i not in sums:
                 sums[i] = [bank(SUM_BANKS[i] + b) for b in range(blocks)]
             for b in range(blocks):
                 nc.tensor.matmul(out=sums[i][b][:, t * P : (t + 1) * P], lhsT=h[t][:, first + b * P : first + (b + 1) * P],
                                  rhs=ident[:], start=True, stop=False, is_transpose=True)
-            taken = take(i, t)
+            take(i, t)
             for b in range(blocks):
-                nc.tensor.matmul(out=sums[i][b][:, t * P : (t + 1) * P], lhsT=taken[:, b * P : (b + 1) * P],
+                nc.tensor.matmul(out=sums[i][b][:, t * P : (t + 1) * P], lhsT=taken[i, t][:, b * P : (b + 1) * P],
                                  rhs=ident[:], start=False, stop=True, is_transpose=True)
 
-        def turn_back(i):
+        def turn_back(i, engine="scalar"):
             first, n = Z_PIECES[i]
             blocks = n // P
-            z_rows = ring.tile([P, blocks * H], BF16, name="z_rows")
-            z_bf[i] = single.tile([P, PACK * n], BF16, name="z_bf_%d" % i, align_bytes=64)
+            z_rows = tile("z_rows_%d" % i, [P, blocks * H], BF16)
+            z_bf[i] = tile("z_bf_%d" % i, [P, PACK * n], BF16)
             back = bank(BACK_BANKS[i])
             for b in range(blocks):
                 nc.scalar.copy(out=z_rows[:, b * H : (b + 1) * H].rearrange("r (u p e) -> r u p e", u=2, e=2),
@@ -199,27 +250,27 @@ def tile_picked_treeup_gelu_e_kernel(tc, xT, w1, w2, share, offs, par, out):
                 for u in range(2):
                     col = (b * 2 + u) * P
                     nc.tensor.transpose(back[:, col : col + P], words[:, u * P : (u + 1) * P], ident[:])
-            nc.scalar.copy(out=z_bf[i][:].bitcast(F32).rearrange("p (b r u) -> p b r u", b=blocks, u=2),
-                           in_=back[:, 0 : 2 * n].rearrange("p (b u r) -> p b r u", b=blocks, u=2))
+            copy(engine, z_bf[i][:].bitcast(F32).rearrange("p (b r u) -> p b r u", b=blocks, u=2),
+                 back[:, 0 : 2 * n].rearrange("p (b u r) -> p b r u", b=blocks, u=2))
 
-        def finish(i, last):
+        def finish(i, engines=None):
             first, n = Z_PIECES[i]
-            blocks = n // P
-            codes = keep.tile([P, n], U32, name="z_codes_%d" % i, align_bytes=64)
-            scales = keep.tile([P, n], U8, name="z_scales_%d" % i, align_bytes=64)
+            codes = tile("z_codes_%d" % i, [P, n], U32)
+            scales = tile("z_scales_%d" % i, [P, n], U8)
             quantize(codes[:], scales[:], z_bf[i][:])
-            result = keep.tile([P, N // P, n], F32, name="result_%d" % i)
+            result = tile("result_%d" % i, [P, N // P, n], F32)
             acc = bank(OUT_BANKS[i])
             for a in range(N // P):
-                if last and a == 1:
+                if engines and a == 1:
                     acc = bank(OUT_BANKS[i] + 1)
-                nc.tensor.matmul_mx(out=acc[:, a * n : (a + 1) * n],
+                col = 0 if engines else a * n
+                nc.tensor.matmul_mx(out=acc[:, col : col + n],
                                     lhsT=w2_codes[:, a * P : (a + 1) * P].bitcast(FP8X4),
                                     lhsT_scale=w2_scales[:, a * P : (a + 1) * P],
                                     rhs=codes[:].bitcast(FP8X4), rhs_scale=scales[:], start=True, stop=True)
-                if last:
-                    copy(("scalar", "vector")[a], result[:, a, :], acc[:, a * n : (a + 1) * n])
-            if not last:
+                if engines:
+                    copy(engines[a], result[:, a, :], acc[:, 0:n])
+            if not engines:
                 nc.scalar.copy(out=result[:].rearrange("p a n -> p (a n)"), in_=acc[:, 0 : 2 * n])
             nc.sync.dma_start(out=out_rows[:, :, first : first + n], in_=result[:])
 
@@ -228,15 +279,15 @@ def tile_picked_treeup_gelu_e_kernel(tc, xT, w1, w2, share, offs, par, out):
             plane_on_tensor(1, t)
         turn_back(0)
         turn_back(1)
-        finish(0, False)
-        for t in range(PACK):
+        finish(0)
+        for t in (3, 2, 1, 0):
             plane_on_tensor(2, t)
-        finish(1, False)
         turn_back(2)
-        for t in range(PACK):
-            plane_on_tensor(3, t)
-        finish(2, False)
-        turn_back(3)
-        finish(3, False)
-        sum_on_vector(4)
-        finish(4, True)
+        finish(1)
+        sum_on_vector(3, (3, 2, 1, 0))
+        weave_z(3, "scalar")
+        finish(2)
+        finish(3)
+        sum_on_vector(4, (3, 2, 1, 0))
+        weave_z(4, "vector")
+        finish(4, ("scalar", "vector"))

@@ -8,6 +8,7 @@ FLOPS = 2 * K * H * S + 2 * H * N * S
 
 F32 = mybir.dt.float32
 BF16 = mybir.dt.bfloat16
+I32 = mybir.dt.int32
 U32 = mybir.dt.uint32
 U16 = mybir.dt.uint16
 U8 = mybir.dt.uint8
@@ -20,36 +21,37 @@ P = 128
 PACK = 4
 STRIPE = 16
 BANK = 512
+RUN = 4
 
 X_LOADS = (
-    ((0, 1024, (("vector", 0, 1024),)),
-     (1024, 512, (("vector", 0, 512),)),
-     (1536, 512, (("vector", 0, 320), ("scalar", 320, 192)))),
-    ((0, 512, (("scalar", 0, 512),)),
-     (512, 512, (("scalar", 0, 512),)),
-     (1024, 512, (("vector", 0, 256), ("scalar", 256, 256))),
-     (1536, 256, (("vector", 0, 256),)),
-     (1792, 256, (("vector", 0, 256),))),
+    ((1024, 1024), (512, 512), (512, 320)),
+    ((512, 0), (512, 0), (512, 256), (256, 256), (256, 160)),
 )
-X_PIECES = ((0, 256, "vector"), (256, 256, "vector"), (512, 256, "scalar"), (768, 256, "scalar"))
-Q_PIECES = ((0, 256), (256, 256), (512, 256), (768, 256))
-EARLY = 1
-H_BANKS = (((0, (0,)), (1, (1,)), (2, (2,)), (3, (3,))), ((4, (0, 1)), (5, (2, 3))), ((6, (0, 1)), (7, (2, 3))), ((0, (0, 1)), (1, (2, 3))))
+
+QUARTER = S // 4
+QUARTERS = (0, 2, 3, 1)
+WOVEN_ON_VECTOR = QUARTERS[:2]
+
 Z_PIECES = ((0, 256), (256, 256), (512, 256), (768, 128), (896, 128))
-SUM_BANKS = {0: 2, 1: 4, 2: 6}
-BACK_BANKS = {0: 0, 1: 1, 2: 2}
-OUT_BANKS = (3, 4, 5, 0, 1)
-AFTER = {"taken_2_2": "taken_0_3", "taken_2_1": "taken_1_3", "taken_2_0": "taken_2_3", "taken_3_3": "taken_2_2", "taken_3_2": "taken_2_1", "taken_3_1": "taken_2_0", "taken_3_0": "taken_3_3", "taken_4_3": "taken_3_2", "taken_4_2": "taken_3_1", "taken_4_1": "taken_3_0", "taken_4_0": "taken_4_3", "x_scales_late": "w1_bf_0", "w2_bf": "x_codes_3", "z_planes_3": "z_bf_0", "z_planes_4": "z_bf_1", "z_codes_4": "z_bf_2"}
+LAST_PIECE = len(Z_PIECES) - 1
+
+OWN_PLACES = 2 * PACK + 1
+RING = 3
+LATE_PLANES = tuple(reversed(range(PACK)))
+
+H_BANKS = (
+    ((0, (0,)), (1, (2,)), (2, (3,)), (3, (1,))),
+    ((2, (2, 3)), (5, (0, 1))),
+    ((1, (2, 3)), (6, (0, 1))),
+    ((0, (2, 3)), (7, (0, 1))),
+)
+SUM_BANKS = (3, 5, 0)
+BACK_BANKS = (2, 7, 3)
+OUT_BANKS = (4, 5, 6, 2, 0)
 
 
 def tile_picked_treeup_gelu_e_kernel(tc, xT, w1, w2, share, offs, par, out):
     nc = tc.nc
-
-    def copy(engine, out, in_):
-        if engine == "vector":
-            nc.vector.tensor_copy(out=out, in_=in_)
-        else:
-            nc.scalar.copy(out=out, in_=in_)
 
     def entries(lst, first, count):
         return lst[:, first // STRIPE : (first + count) // STRIPE]
@@ -57,15 +59,18 @@ def tile_picked_treeup_gelu_e_kernel(tc, xT, w1, w2, share, offs, par, out):
     def quantize(codes, scales, values):
         nc.vector.quantize_mx(out=codes.bitcast(FP8X4), scales=scales, in_=values)
 
+    def product(acc, w_codes, w_scales, column, codes, scales):
+        nc.tensor.matmul_mx(out=acc, lhsT=w_codes[:, column : column + P].bitcast(FP8X4),
+                            lhsT_scale=w_scales[:, column : column + P],
+                            rhs=codes[:].bitcast(FP8X4), rhs_scale=scales[:], start=True, stop=True)
+
     with ExitStack() as ctx:
         lists = ctx.enter_context(tc.tile_pool(name="lists", bufs=1))
         keep = ctx.enter_context(tc.tile_pool(name="keep", bufs=1))
         psum = ctx.enter_context(tc.psum_pool(name="psum", bufs=1))
 
-        def tile(name, shape, dtype):
-            while name in AFTER:
-                name = AFTER[name]
-            return keep.tile(shape, dtype, name=name, align_bytes=64)
+        def tile(name, shape, dtype, place_of=None):
+            return keep.tile(shape, dtype, name=name, tag=place_of or name, align_bytes=64)
 
         def bank(number):
             return psum.tile([P, BANK], F32, name="bank_%d" % number)
@@ -73,22 +78,25 @@ def tile_picked_treeup_gelu_e_kernel(tc, xT, w1, w2, share, offs, par, out):
         offs_t = lists.tile([P, S // STRIPE], U16, name="offs_t")
         par_t = lists.tile([P, S // STRIPE], U16, name="par_t")
 
-        warm_in = tile("warm_in", [P, 8], F32)
-        warm_out = tile("warm_out", [P, 8], F32)
-        nc.vector.memset(warm_in[:], 0.0)
-        nc.scalar.activation(out=warm_out[:], in_=warm_in[:], func=GELU)
+        zero = tile("zero", [P, 1], F32)
+        no_bias = tile("no_bias", [P, 1], F32)
+        nc.vector.memset(zero[:], 0.0)
+        nc.scalar.activation(out=no_bias[:], in_=zero[:], func=GELU)
 
         ident = tile("ident", [P, P], F32)
         make_identity(nc, ident[:])
 
-        x_rows = xT.rearrange("(p j) t -> p j t", j=PACK)
-        raw = {}
+        x_rows = xT.rearrange("(p j) c -> p j c", j=PACK)
+        x_raw = ([], [])
         for u in range(2):
-            for first, cols, shares in X_LOADS[u]:
-                raw[u, first] = tile("x_raw_%d_%d" % (u, first), [P, 2, cols], F32)
-                nc.sync.dma_start(out=raw[u, first][:], in_=x_rows[:, 2 * u : 2 * u + 2, first : first + cols])
+            first = 0
+            for cols, on_vector in X_LOADS[u]:
+                raw = tile("x_raw_%d_%d" % (u, first), [P, 2, cols], F32)
+                nc.sync.dma_start(out=raw[:], in_=x_rows[:, 2 * u : 2 * u + 2, first : first + cols])
                 if (u, first) == (0, 0):
                     nc.sync.dma_start(offs_t[:], offs)
+                x_raw[u].append((raw, first, cols, on_vector))
+                first = first + cols
         w1_rows = w1.rearrange("(p j) c -> p j c", j=PACK)
         w1_raw = []
         for half in range(2):
@@ -98,196 +106,162 @@ def tile_picked_treeup_gelu_e_kernel(tc, xT, w1, w2, share, offs, par, out):
         nc.sync.dma_start(out=share_t[:], in_=share)
         nc.sync.dma_start(par_t[:], par)
         w2_raw = tile("w2_raw", [P, PACK, N], F32)
-        nc.sync.dma_start(out=w2_raw[:], in_=w2.rearrange("(p j) n -> p j n", j=PACK))
+        nc.sync.dma_start(out=w2_raw[:], in_=w2.rearrange("(p j) c -> p j c", j=PACK))
 
         pairs = [tile("pairs_%d" % u, [P, T], U32) for u in range(2)]
-        x_bf, x_flat, x_codes, x_scales = {}, {}, {}, {}
+        picked = {q: tile("picked_%d" % q, [P, 2 * QUARTER], U32) for q in QUARTERS}
+        for u in range(2):
+            halves = pairs[u][:].bitcast(BF16).rearrange("p (c e) -> p c e", e=2)
+            for raw, first, cols, on_vector in x_raw[u]:
+                rows = raw[:].rearrange("p e c -> p c e")
+                if on_vector > 0:
+                    nc.vector.tensor_copy(out=halves[:, first : first + on_vector, :], in_=rows[:, 0:on_vector, :])
+                if on_vector < cols:
+                    nc.scalar.copy(out=halves[:, first + on_vector : first + cols, :], in_=rows[:, on_vector:cols, :])
+            for q in QUARTERS:
+                nc.vector.tensor_copy(out=picked[q][:, u * QUARTER : (u + 1) * QUARTER],
+                                      in_=pairs[u][:].indirect(entries(offs_t, q * QUARTER, QUARTER)))
 
-        def pair_up(u):
-            view = pairs[u][:].bitcast(BF16).rearrange("p (t e) -> p t e", e=2)
-            for first, cols, shares in X_LOADS[u]:
-                for engine, start, count in shares:
-                    copy(engine, view[:, first + start : first + start + count, :],
-                         raw[u, first][:, :, start : start + count].rearrange("p e t -> p t e"))
+        x_bf, x_codes, x_scales = {}, {}, {}
 
-        def pick(u, i):
-            first, n, weaver = X_PIECES[i]
-            if weaver is None:
-                if u == 0:
-                    x_bf[i] = tile("x_bf_%d" % i, [P, PACK * n], BF16)
-                words = x_bf[i][:].bitcast(U32).rearrange("p (t u) -> p t u", u=2)
-                nc.vector.tensor_copy(out=words[:, :, u], in_=pairs[u][:].indirect(entries(offs_t, first, n)))
-            else:
-                if u == 0:
-                    x_flat[i] = tile("x_flat_%d" % i, [P, 2 * n], U32)
-                nc.vector.tensor_copy(out=x_flat[i][:, u * n : (u + 1) * n], in_=pairs[u][:].indirect(entries(offs_t, first, n)))
-
-        def weave_x(i):
-            first, n, weaver = X_PIECES[i]
-            x_bf[i] = tile("x_bf_%d" % i, [P, PACK * n], BF16)
-            dt = U32 if weaver == "scalar" else mybir.dt.int32
-            copy(weaver, x_bf[i][:].bitcast(dt).rearrange("p (t u) -> p t u", u=2),
-                 x_flat[i][:].bitcast(dt).rearrange("p (u t) -> p t u", u=2))
-
-        late = {}
+        def weave_x(q):
+            word = I32 if q in WOVEN_ON_VECTOR else U32
+            move = nc.vector.tensor_copy if q in WOVEN_ON_VECTOR else nc.scalar.copy
+            move(out=x_bf[q].bitcast(word).rearrange("p (c u) -> p c u", u=2),
+                 in_=picked[q][:].bitcast(word).rearrange("p (u c) -> p c u", u=2))
 
         def quantize_x(q):
-            first, n = Q_PIECES[q]
-            i = [i for i, piece in enumerate(X_PIECES) if piece[0] <= first][-1]
-            x_codes[q] = tile("x_codes_%d" % q, [P, n], U32)[:]
-            if q < EARLY:
-                x_scales[q] = tile("x_scales_%d" % q, [P, n], U8)[:]
-            else:
-                if not late:
-                    late[0] = tile("x_scales_late", [P, S], U8)
-                x_scales[q] = late[0][:, first : first + n]
-            lo = first - X_PIECES[i][0]
-            quantize(x_codes[q], x_scales[q], x_bf[i][:, PACK * lo : PACK * (lo + n)])
+            x_codes[q] = tile("x_codes_%d" % q, [P, QUARTER], U32)
+            x_scales[q] = tile("x_scales_%d" % q, [P, QUARTER], U8)
+            quantize(x_codes[q][:], x_scales[q][:], x_bf[q])
+
+        x_bf[QUARTERS[0]] = tile("x_bf_first", [P, PACK * QUARTER], BF16)[:]
+        weave_x(QUARTERS[0])
 
         w1_bf = [tile("w1_bf_%d" % v, [P, 2, P, PACK], BF16) for v in range(2)]
+        for half in range(2):
+            for v in range(2):
+                nc.scalar.copy(
+                    out=w1_bf[v][:, :, half * (P // 2) : (half + 1) * (P // 2), :].rearrange("p e m j -> p m j e"),
+                    in_=w1_raw[half][:].rearrange("p j (m t) -> p m j t", t=PACK)[:, :, :, 2 * v : 2 * v + 2])
         w1_codes, w1_scales = {}, {}
-
-        def weave_w1(half, v, engine):
-            copy(engine, w1_bf[v][:, :, half * (P // 2) : (half + 1) * (P // 2), :].rearrange("p t m j -> p m j t"),
-                 w1_raw[half][:].rearrange("p j (m t) -> p m j t", t=PACK)[:, :, :, 2 * v : 2 * v + 2])
 
         def quantize_w1(v):
             w1_codes[v] = tile("w1_codes_%d" % v, [P, 2 * P], U32)
             w1_scales[v] = tile("w1_scales_%d" % v, [P, 2 * P], U8)
-            quantize(w1_codes[v][:], w1_scales[v][:], w1_bf[v][:].rearrange("p t m j -> p (t m j)"))
+            quantize(w1_codes[v][:], w1_scales[v][:], w1_bf[v][:].rearrange("p e m j -> p (e m j)"))
 
-        pair_up(0)
-        for i in range(len(X_PIECES)):
-            pick(0, i)
-        pair_up(1)
-        for i in range(len(X_PIECES)):
-            pick(1, i)
-        weave_x(0)
-        weave_x(1)
-        weave_w1(0, 0, "scalar")
-        weave_w1(0, 1, "scalar")
-        weave_w1(1, 0, "scalar")
-        weave_x(2)
-        weave_x(3)
-        weave_w1(1, 1, "scalar")
-        quantize_x(0)
+        quantize_x(QUARTERS[0])
         quantize_w1(0)
-        for q in (1, 2, 3):
-            quantize_x(q)
+        x_bf_late = tile("x_bf_late", [P, PACK * (S - QUARTER)], BF16, place_of="w1_raw_1")
+        for q in QUARTERS[1:]:
+            x_bf[q] = x_bf_late[:, PACK * QUARTER * (q - 1) : PACK * QUARTER * q]
+            weave_x(q)
         quantize_w1(1)
+        for q in QUARTERS[1:]:
+            quantize_x(q)
 
-        h = [tile("h_%d" % t, [P, S], F32) for t in range(PACK)]
-        for t in range(PACK):
-            for number, members in H_BANKS[t]:
-                acc = bank(number)
-                start = Q_PIECES[members[0]][0]
-                for i in members:
-                    first, n = Q_PIECES[i]
-                    nc.tensor.matmul_mx(out=acc[:, first - start : first - start + n],
-                                        lhsT=w1_codes[t // 2][:, (t % 2) * P : (t % 2 + 1) * P].bitcast(FP8X4),
-                                        lhsT_scale=w1_scales[t // 2][:, (t % 2) * P : (t % 2 + 1) * P],
-                                        rhs=x_codes[i].bitcast(FP8X4), rhs_scale=x_scales[i], start=True, stop=True)
-                nc.scalar.activation(out=h[t][:, start : first + n], in_=acc[:, 0 : first + n - start], func=GELU)
-
-        w2_bf = tile("w2_bf", [P, N, PACK], BF16)
-        copy("scalar", w2_bf[:].rearrange("p (c i) j -> p c j i", i=4), w2_raw[:].rearrange("p j (c i) -> p c j i", i=4))
+        w2_bf = tile("w2_bf", [P, N, PACK], BF16, place_of="w1_raw_1")
+        nc.vector.tensor_copy(out=w2_bf[:].rearrange("p (c i) j -> p c j i", i=RUN),
+                              in_=w2_raw[:].rearrange("p j (c i) -> p c j i", i=RUN))
         w2_codes = tile("w2_codes", [P, N], U32)
         w2_scales = tile("w2_scales", [P, N], U8)
 
-        quantize(w2_codes[:], w2_scales[:], w2_bf[:].rearrange("p n j -> p (n j)"))
+        h = [tile("h_%d" % t, [P, S], F32) for t in range(PACK)]
+        for t in range(PACK):
+            for number, quarters in H_BANKS[t]:
+                acc = bank(number)
+                for place, q in enumerate(quarters):
+                    product(acc[:, place * QUARTER : (place + 1) * QUARTER], w1_codes[t // 2], w1_scales[t // 2],
+                            (t % 2) * P, x_codes[q], x_scales[q])
+                first, n = quarters[0] * QUARTER, len(quarters) * QUARTER
+                nc.scalar.activation(out=h[t][:, first : first + n], in_=acc[:, 0:n], func=GELU, bias=no_bias[:])
 
-        out_rows = out.rearrange("(a p) j -> p a j", p=P)
-        z_bf, sums, planes, taken = {}, {}, {}, {}
+        quantize(w2_codes[:], w2_scales[:], w2_bf[:].rearrange("p c j -> p (c j)"))
+
+        out_rows = out.rearrange("(a p) c -> p a c", p=P)
+        z_bf, sums, places = {}, {}, []
 
         def take(i, t):
             first, n = Z_PIECES[i]
-            taken[i, t] = tile("taken_%d_%d" % (i, t), [P, n], F32)
-            nc.vector.tensor_tensor(out=taken[i, t][:], in0=h[t][:].indirect(entries(par_t, first, n)),
+            name = "taken_%d_%d" % (i, t)
+            places.append(name if len(places) < OWN_PLACES else places[-RING])
+            taken = tile(name, [P, n], F32, place_of=places[-1])
+            nc.vector.tensor_tensor(out=taken[:], in0=h[t][:].indirect(entries(par_t, first, n)),
                                     in1=share_t[:, first : first + n], op=MULT)
+            return taken
 
-        def add(i, t):
+        def add_on_tensor(i, t):
             first, n = Z_PIECES[i]
-            if i not in planes:
-                planes[i] = tile("z_planes_%d" % i, [P, PACK, n], BF16)
-            nc.vector.tensor_tensor(out=planes[i][:, t, :], in0=taken[i, t][:], in1=h[t][:, first : first + n], op=ADD)
-
-        def weave_z(i, engine):
-            first, n = Z_PIECES[i]
-            z_bf[i] = tile("z_bf_%d" % i, [P, PACK * n], BF16)
-            copy(engine, z_bf[i][:].rearrange("p (c i t) -> p c t i", i=4, t=PACK),
-                 planes[i][:].rearrange("p t (c i) -> p c t i", i=4))
-
-        def sum_on_vector(i, order):
-            take(i, order[0])
-            for s, t in enumerate(order):
-                if s + 1 < PACK:
-                    take(i, order[s + 1])
-                add(i, t)
-
-        def plane_on_tensor(i, t):
-            first, n = Z_PIECES[i]
-            blocks = n // P
             if i not in sums:
-                sums[i] = [bank(SUM_BANKS[i] + b) for b in range(blocks)]
-            for b in range(blocks):
-                nc.tensor.matmul(out=sums[i][b][:, t * P : (t + 1) * P], lhsT=h[t][:, first + b * P : first + (b + 1) * P],
+                sums[i] = [bank(SUM_BANKS[i] + b) for b in range(n // P)]
+            for b in range(n // P):
+                nc.tensor.matmul(out=sums[i][b][:, t * P : (t + 1) * P],
+                                 lhsT=h[t][:, first + b * P : first + (b + 1) * P],
                                  rhs=ident[:], start=True, stop=False, is_transpose=True)
-            take(i, t)
-            for b in range(blocks):
-                nc.tensor.matmul(out=sums[i][b][:, t * P : (t + 1) * P], lhsT=taken[i, t][:, b * P : (b + 1) * P],
+            taken = take(i, t)
+            for b in range(n // P):
+                nc.tensor.matmul(out=sums[i][b][:, t * P : (t + 1) * P], lhsT=taken[:, b * P : (b + 1) * P],
                                  rhs=ident[:], start=False, stop=True, is_transpose=True)
 
-        def turn_back(i, engine="scalar"):
+        def turn_back(i):
             first, n = Z_PIECES[i]
             blocks = n // P
             z_rows = tile("z_rows_%d" % i, [P, blocks * H], BF16)
             z_bf[i] = tile("z_bf_%d" % i, [P, PACK * n], BF16)
             back = bank(BACK_BANKS[i])
             for b in range(blocks):
-                nc.scalar.copy(out=z_rows[:, b * H : (b + 1) * H].rearrange("r (u p e) -> r u p e", u=2, e=2),
+                row = z_rows[:, b * H : (b + 1) * H]
+                nc.scalar.copy(out=row.rearrange("r (u p e) -> r u p e", u=2, e=2),
                                in_=sums[i][b][:].rearrange("r (u e p) -> r u p e", u=2, e=2))
-                words = z_rows[:, b * H : (b + 1) * H].bitcast(F32)
                 for u in range(2):
-                    col = (b * 2 + u) * P
-                    nc.tensor.transpose(back[:, col : col + P], words[:, u * P : (u + 1) * P], ident[:])
-            copy(engine, z_bf[i][:].bitcast(F32).rearrange("p (b r u) -> p b r u", b=blocks, u=2),
-                 back[:, 0 : 2 * n].rearrange("p (b u r) -> p b r u", b=blocks, u=2))
+                    column = (2 * b + u) * P
+                    nc.tensor.transpose(back[:, column : column + P], row.bitcast(F32)[:, u * P : (u + 1) * P], ident[:])
+            nc.scalar.copy(out=z_bf[i][:].bitcast(F32).rearrange("p (b r u) -> p b r u", b=blocks, u=2),
+                           in_=back[:].rearrange("p (b u r) -> p b r u", b=blocks, u=2))
 
-        def finish(i, engines=None):
+        def sum_on_vector(i, weave):
             first, n = Z_PIECES[i]
-            codes = tile("z_codes_%d" % i, [P, n], U32)
+            taken = take(i, LATE_PLANES[0])
+            planes = tile("z_planes_%d" % i, [P, PACK, n], BF16, place_of="z_bf_%d" % (i - 3))
+            for step, t in enumerate(LATE_PLANES):
+                following = take(i, LATE_PLANES[step + 1]) if step + 1 < PACK else None
+                nc.vector.tensor_tensor(out=planes[:, t, :], in0=taken[:], in1=h[t][:, first : first + n], op=ADD)
+                taken = following
+            z_bf[i] = tile("z_bf_%d" % i, [P, PACK * n], BF16)
+            weave(out=z_bf[i][:].rearrange("p (c i t) -> p c t i", i=RUN, t=PACK),
+                  in_=planes[:].rearrange("p t (c i) -> p c t i", i=RUN))
+
+        def finish(i):
+            first, n = Z_PIECES[i]
+            codes = tile("z_codes_%d" % i, [P, n], U32, place_of="z_bf_%d" % (i - 2) if i == LAST_PIECE else None)
             scales = tile("z_scales_%d" % i, [P, n], U8)
             quantize(codes[:], scales[:], z_bf[i][:])
             result = tile("result_%d" % i, [P, N // P, n], F32)
-            acc = bank(OUT_BANKS[i])
-            for a in range(N // P):
-                if engines and a == 1:
-                    acc = bank(OUT_BANKS[i] + 1)
-                col = 0 if engines else a * n
-                nc.tensor.matmul_mx(out=acc[:, col : col + n],
-                                    lhsT=w2_codes[:, a * P : (a + 1) * P].bitcast(FP8X4),
-                                    lhsT_scale=w2_scales[:, a * P : (a + 1) * P],
-                                    rhs=codes[:].bitcast(FP8X4), rhs_scale=scales[:], start=True, stop=True)
-                if engines:
-                    copy(engines[a], result[:, a, :], acc[:, 0:n])
-            if not engines:
-                nc.scalar.copy(out=result[:].rearrange("p a n -> p (a n)"), in_=acc[:, 0 : 2 * n])
+            if i == LAST_PIECE:
+                for a, move in enumerate((nc.scalar.copy, nc.vector.tensor_copy)):
+                    acc = bank(OUT_BANKS[i] + a)
+                    product(acc[:, 0:n], w2_codes, w2_scales, a * P, codes, scales)
+                    move(out=result[:, a, :], in_=acc[:, 0:n])
+            else:
+                acc = bank(OUT_BANKS[i])
+                for a in range(N // P):
+                    product(acc[:, a * n : (a + 1) * n], w2_codes, w2_scales, a * P, codes, scales)
+                nc.scalar.copy(out=result[:].rearrange("p a c -> p (a c)"), in_=acc[:, 0 : (N // P) * n])
             nc.sync.dma_start(out=out_rows[:, :, first : first + n], in_=result[:])
 
         for t in range(PACK):
-            plane_on_tensor(0, t)
-            plane_on_tensor(1, t)
+            add_on_tensor(0, t)
+            add_on_tensor(1, t)
         turn_back(0)
         turn_back(1)
         finish(0)
-        for t in (3, 2, 1, 0):
-            plane_on_tensor(2, t)
+        for t in LATE_PLANES:
+            add_on_tensor(2, t)
         turn_back(2)
         finish(1)
-        sum_on_vector(3, (3, 2, 1, 0))
-        weave_z(3, "scalar")
+        sum_on_vector(3, nc.scalar.copy)
         finish(2)
         finish(3)
-        sum_on_vector(4, (3, 2, 1, 0))
-        weave_z(4, "vector")
-        finish(4, ("scalar", "vector"))
+        sum_on_vector(4, nc.vector.tensor_copy)
+        finish(4)

@@ -31,23 +31,21 @@ X_LOADS = (
 QUARTER = S // 4
 QUARTERS = (0, 2, 3, 1)
 WOVEN_ON_VECTOR = QUARTERS[:2]
+WOVEN_ON_SCALAR = QUARTERS[2:]
 
 Z_PIECES = ((0, 256), (256, 256), (512, 256), (768, 128), (896, 128))
+LAST_ON_TENSOR = 2
 LAST_PIECE = len(Z_PIECES) - 1
-
-OWN_PLACES = 2 * PACK + 1
-RING = 3
-LATE_PLANES = tuple(reversed(range(PACK)))
 
 H_BANKS = (
     ((0, (0,)), (1, (2,)), (2, (3,)), (3, (1,))),
-    ((2, (2, 3)), (5, (0, 1))),
-    ((1, (2, 3)), (6, (0, 1))),
-    ((0, (2, 3)), (7, (0, 1))),
+    ((0, (2, 3)), (1, (0, 1))),
+    ((4, (0, 1)), (5, (2, 3))),
+    ((6, (0, 1)), (7, (2, 3))),
 )
-SUM_BANKS = (3, 5, 0)
-BACK_BANKS = (2, 7, 3)
-OUT_BANKS = (4, 5, 6, 2, 0)
+SUM_BANKS = (2, 0, 4)
+BACK_BANKS = (6, 7, 2)
+OUT_BANKS = (3, 5, 0, 6, 3)
 
 
 def tile_picked_treeup_gelu_e_kernel(tc, xT, w1, w2, share, offs, par, out):
@@ -102,8 +100,11 @@ def tile_picked_treeup_gelu_e_kernel(tc, xT, w1, w2, share, offs, par, out):
         for half in range(2):
             w1_raw.append(tile("w1_raw_%d" % half, [P, PACK, H // 2], F32))
             nc.sync.dma_start(out=w1_raw[half][:], in_=w1_rows[:, :, half * (H // 2) : (half + 1) * (H // 2)])
-        share_t = tile("share_t", [P, S], F32)
-        nc.sync.dma_start(out=share_t[:], in_=share)
+        head = Z_PIECES[0][1]
+        share_head = tile("share_head", [P, head], F32)
+        share_rest = tile("share_rest", [P, S - head], F32)
+        nc.sync.dma_start(out=share_head[:], in_=share[:, 0:head])
+        nc.sync.dma_start(out=share_rest[:], in_=share[:, head:S])
         nc.sync.dma_start(par_t[:], par)
         w2_raw = tile("w2_raw", [P, PACK, N], F32)
         nc.sync.dma_start(out=w2_raw[:], in_=w2.rearrange("(p j) c -> p j c", j=PACK))
@@ -135,35 +136,40 @@ def tile_picked_treeup_gelu_e_kernel(tc, xT, w1, w2, share, offs, par, out):
             x_scales[q] = tile("x_scales_%d" % q, [P, QUARTER], U8)
             quantize(x_codes[q][:], x_scales[q][:], x_bf[q])
 
-        x_bf[QUARTERS[0]] = tile("x_bf_first", [P, PACK * QUARTER], BF16)[:]
-        weave_x(QUARTERS[0])
+        for q in WOVEN_ON_VECTOR:
+            x_bf[q] = tile("x_bf_%d" % q, [P, PACK * QUARTER], BF16)[:]
+            weave_x(q)
 
         w1_bf = [tile("w1_bf_%d" % v, [P, 2, P, PACK], BF16) for v in range(2)]
-        for half in range(2):
-            for v in range(2):
-                nc.scalar.copy(
-                    out=w1_bf[v][:, :, half * (P // 2) : (half + 1) * (P // 2), :].rearrange("p e m j -> p m j e"),
-                    in_=w1_raw[half][:].rearrange("p j (m t) -> p m j t", t=PACK)[:, :, :, 2 * v : 2 * v + 2])
         w1_codes, w1_scales = {}, {}
+
+        def weave_w1(half, v):
+            nc.scalar.copy(
+                out=w1_bf[v][:, :, half * (P // 2) : (half + 1) * (P // 2), :].rearrange("p e m j -> p m j e"),
+                in_=w1_raw[half][:].rearrange("p j (m t) -> p m j t", t=PACK)[:, :, :, 2 * v : 2 * v + 2])
 
         def quantize_w1(v):
             w1_codes[v] = tile("w1_codes_%d" % v, [P, 2 * P], U32)
             w1_scales[v] = tile("w1_scales_%d" % v, [P, 2 * P], U8)
             quantize(w1_codes[v][:], w1_scales[v][:], w1_bf[v][:].rearrange("p e m j -> p (e m j)"))
 
+        weave_w1(0, 0)
+        weave_w1(0, 1)
+        weave_w1(1, 0)
+        x_bf_late = tile("x_bf_late", [P, len(WOVEN_ON_SCALAR) * PACK * QUARTER], BF16, place_of="w1_raw_0")
+        for nth, q in enumerate(WOVEN_ON_SCALAR):
+            x_bf[q] = x_bf_late[:, PACK * QUARTER * nth : PACK * QUARTER * (nth + 1)]
+            weave_x(q)
+        weave_w1(1, 1)
         quantize_x(QUARTERS[0])
         quantize_w1(0)
-        x_bf_late = tile("x_bf_late", [P, PACK * (S - QUARTER)], BF16, place_of="w1_raw_1")
-        for q in QUARTERS[1:]:
-            x_bf[q] = x_bf_late[:, PACK * QUARTER * (q - 1) : PACK * QUARTER * q]
-            weave_x(q)
-        quantize_w1(1)
         for q in QUARTERS[1:]:
             quantize_x(q)
+        quantize_w1(1)
 
-        w2_bf = tile("w2_bf", [P, N, PACK], BF16, place_of="w1_raw_1")
-        nc.vector.tensor_copy(out=w2_bf[:].rearrange("p (c i) j -> p c j i", i=RUN),
-                              in_=w2_raw[:].rearrange("p j (c i) -> p c j i", i=RUN))
+        w2_bf = tile("w2_bf", [P, N, PACK], BF16, place_of="w1_raw_0")
+        nc.vector.tensor_copy(out=w2_bf[:].rearrange("p (c d) j -> p c j d", d=RUN),
+                              in_=w2_raw[:].rearrange("p j (c d) -> p c j d", d=RUN))
         w2_codes = tile("w2_codes", [P, N], U32)
         w2_scales = tile("w2_scales", [P, N], U8)
 
@@ -171,8 +177,8 @@ def tile_picked_treeup_gelu_e_kernel(tc, xT, w1, w2, share, offs, par, out):
         for t in range(PACK):
             for number, quarters in H_BANKS[t]:
                 acc = bank(number)
-                for place, q in enumerate(quarters):
-                    product(acc[:, place * QUARTER : (place + 1) * QUARTER], w1_codes[t // 2], w1_scales[t // 2],
+                for nth, q in enumerate(quarters):
+                    product(acc[:, nth * QUARTER : (nth + 1) * QUARTER], w1_codes[t // 2], w1_scales[t // 2],
                             (t % 2) * P, x_codes[q], x_scales[q])
                 first, n = quarters[0] * QUARTER, len(quarters) * QUARTER
                 nc.scalar.activation(out=h[t][:, first : first + n], in_=acc[:, 0:n], func=GELU, bias=no_bias[:])
@@ -180,88 +186,103 @@ def tile_picked_treeup_gelu_e_kernel(tc, xT, w1, w2, share, offs, par, out):
         quantize(w2_codes[:], w2_scales[:], w2_bf[:].rearrange("p c j -> p (c j)"))
 
         out_rows = out.rearrange("(a p) c -> p a c", p=P)
-        z_bf, sums, places = {}, {}, []
+        z_bf, sums = {}, {}
 
-        def take(i, t):
-            first, n = Z_PIECES[i]
-            name = "taken_%d_%d" % (i, t)
-            places.append(name if len(places) < OWN_PLACES else places[-RING])
-            taken = tile(name, [P, n], F32, place_of=places[-1])
-            nc.vector.tensor_tensor(out=taken[:], in0=h[t][:].indirect(entries(par_t, first, n)),
-                                    in1=share_t[:, first : first + n], op=MULT)
-            return taken
+        def take(piece, t, taken):
+            first, n = Z_PIECES[piece]
+            factors = share_head[:] if piece == 0 else share_rest[:, first - head : first - head + n]
+            nc.vector.tensor_tensor(out=taken, in0=h[t][:].indirect(entries(par_t, first, n)), in1=factors, op=MULT)
 
-        def add_on_tensor(i, t):
-            first, n = Z_PIECES[i]
-            if i not in sums:
-                sums[i] = [bank(SUM_BANKS[i] + b) for b in range(n // P)]
-            for b in range(n // P):
-                nc.tensor.matmul(out=sums[i][b][:, t * P : (t + 1) * P],
-                                 lhsT=h[t][:, first + b * P : first + (b + 1) * P],
-                                 rhs=ident[:], start=True, stop=False, is_transpose=True)
-            taken = take(i, t)
-            for b in range(n // P):
-                nc.tensor.matmul(out=sums[i][b][:, t * P : (t + 1) * P], lhsT=taken[:, b * P : (b + 1) * P],
-                                 rhs=ident[:], start=False, stop=True, is_transpose=True)
+        def open_sums(piece):
+            sums[piece] = [bank(SUM_BANKS[piece] + b) for b in range(Z_PIECES[piece][1] // P)]
 
-        def turn_back(i):
-            first, n = Z_PIECES[i]
-            blocks = n // P
-            z_rows = tile("z_rows_%d" % i, [P, blocks * H], BF16)
-            z_bf[i] = tile("z_bf_%d" % i, [P, PACK * n], BF16)
-            back = bank(BACK_BANKS[i])
-            for b in range(blocks):
+        def transpose_own(piece, b, t):
+            first = Z_PIECES[piece][0] + b * P
+            nc.tensor.matmul(out=sums[piece][b][:, t * P : (t + 1) * P], lhsT=h[t][:, first : first + P],
+                             rhs=ident[:], start=True, stop=False, is_transpose=True)
+
+        def transpose_taken(piece, b, t, taken):
+            nc.tensor.matmul(out=sums[piece][b][:, t * P : (t + 1) * P], lhsT=taken[:, b * P : (b + 1) * P],
+                             rhs=ident[:], start=False, stop=True, is_transpose=True)
+
+        def turn_back(piece):
+            first, n = Z_PIECES[piece]
+            batches = n // P
+            z_rows = tile("z_rows_%d" % piece, [P, batches * H], BF16)
+            z_bf[piece] = tile("z_bf_%d" % piece, [P, PACK * n], BF16)
+            back = bank(BACK_BANKS[piece])
+            for b in range(batches):
                 row = z_rows[:, b * H : (b + 1) * H]
                 nc.scalar.copy(out=row.rearrange("r (u p e) -> r u p e", u=2, e=2),
-                               in_=sums[i][b][:].rearrange("r (u e p) -> r u p e", u=2, e=2))
+                               in_=sums[piece][b][:].rearrange("r (u e p) -> r u p e", u=2, e=2))
                 for u in range(2):
                     column = (2 * b + u) * P
-                    nc.tensor.transpose(back[:, column : column + P], row.bitcast(F32)[:, u * P : (u + 1) * P], ident[:])
-            nc.scalar.copy(out=z_bf[i][:].bitcast(F32).rearrange("p (b r u) -> p b r u", b=blocks, u=2),
-                           in_=back[:].rearrange("p (b u r) -> p b r u", b=blocks, u=2))
+                    nc.tensor.transpose(back[:, column : column + P], row.bitcast(F32)[:, u * P : (u + 1) * P],
+                                        ident[:])
+            nc.scalar.copy(out=z_bf[piece][:].bitcast(F32).rearrange("p (b r u) -> p b r u", b=batches, u=2),
+                           in_=back[:].rearrange("p (b u r) -> p b r u", b=batches, u=2))
 
-        def sum_on_vector(i, weave):
-            first, n = Z_PIECES[i]
-            taken = take(i, LATE_PLANES[0])
-            planes = tile("z_planes_%d" % i, [P, PACK, n], BF16, place_of="z_bf_%d" % (i - 3))
-            for step, t in enumerate(LATE_PLANES):
-                following = take(i, LATE_PLANES[step + 1]) if step + 1 < PACK else None
-                nc.vector.tensor_tensor(out=planes[:, t, :], in0=taken[:], in1=h[t][:, first : first + n], op=ADD)
-                taken = following
-            z_bf[i] = tile("z_bf_%d" % i, [P, PACK * n], BF16)
-            weave(out=z_bf[i][:].rearrange("p (c i t) -> p c t i", i=RUN, t=PACK),
-                  in_=planes[:].rearrange("p t (c i) -> p c t i", i=RUN))
+        def sum_on_vector(piece, taken, weave, planes_in_place_of=None):
+            first, n = Z_PIECES[piece]
+            take(piece, 0, taken[:, 0, :])
+            planes = tile("z_planes_%d" % piece, [P, PACK, n], BF16, place_of=planes_in_place_of)
+            for t in range(PACK):
+                if t + 1 < PACK:
+                    take(piece, t + 1, taken[:, t + 1, :])
+                nc.vector.tensor_tensor(out=planes[:, t, :], in0=taken[:, t, :], in1=h[t][:, first : first + n], op=ADD)
+            z_bf[piece] = tile("z_bf_%d" % piece, [P, PACK * n], BF16)
+            weave(out=z_bf[piece][:].rearrange("p (c d t) -> p c t d", d=RUN, t=PACK),
+                  in_=planes[:].rearrange("p t (c d) -> p c t d", d=RUN))
 
-        def finish(i):
-            first, n = Z_PIECES[i]
-            codes = tile("z_codes_%d" % i, [P, n], U32, place_of="z_bf_%d" % (i - 2) if i == LAST_PIECE else None)
-            scales = tile("z_scales_%d" % i, [P, n], U8)
-            quantize(codes[:], scales[:], z_bf[i][:])
-            result = tile("result_%d" % i, [P, N // P, n], F32)
-            if i == LAST_PIECE:
+        def finish(piece, codes_in_place_of=None):
+            first, n = Z_PIECES[piece]
+            codes = tile("z_codes_%d" % piece, [P, n], U32, place_of=codes_in_place_of)
+            scales = tile("z_scales_%d" % piece, [P, n], U8)
+            quantize(codes[:], scales[:], z_bf[piece][:])
+            result = tile("result_%d" % piece, [P, N // P, n], F32)
+            if piece in (LAST_ON_TENSOR, LAST_PIECE):
                 for a, move in enumerate((nc.scalar.copy, nc.vector.tensor_copy)):
-                    acc = bank(OUT_BANKS[i] + a)
+                    acc = bank(OUT_BANKS[piece] + a)
                     product(acc[:, 0:n], w2_codes, w2_scales, a * P, codes, scales)
                     move(out=result[:, a, :], in_=acc[:, 0:n])
             else:
-                acc = bank(OUT_BANKS[i])
+                acc = bank(OUT_BANKS[piece])
                 for a in range(N // P):
                     product(acc[:, a * n : (a + 1) * n], w2_codes, w2_scales, a * P, codes, scales)
                 nc.scalar.copy(out=result[:].rearrange("p a c -> p (a c)"), in_=acc[:, 0 : (N // P) * n])
             nc.sync.dma_start(out=out_rows[:, :, first : first + n], in_=result[:])
 
         for t in range(PACK):
-            add_on_tensor(0, t)
-            add_on_tensor(1, t)
+            for piece in range(2):
+                if t == 0:
+                    open_sums(piece)
+                for b in range(len(sums[piece])):
+                    transpose_own(piece, b, t)
+                taken = tile("taken_%d_%d" % (piece, t), [P, Z_PIECES[piece][1]], F32)
+                take(piece, t, taken[:])
+                for b in range(len(sums[piece])):
+                    transpose_taken(piece, b, t, taken)
         turn_back(0)
         turn_back(1)
         finish(0)
-        for t in LATE_PLANES:
-            add_on_tensor(2, t)
+
+        wide, narrow = Z_PIECES[2][1], Z_PIECES[3][1]
+        taken_middle = tile("taken_middle", [P, PACK * (wide + narrow)], F32, place_of="share_head")
+        taken_2 = taken_middle[:, 0 : PACK * wide].rearrange("p (t c) -> p t c", t=PACK)
+        taken_3 = taken_middle[:, PACK * wide : PACK * (wide + narrow)].rearrange("p (t c) -> p t c", t=PACK)
+        for t in range(PACK):
+            take(2, t, taken_2[:, t, :])
+        open_sums(2)
+        for b in range(len(sums[2])):
+            for t in range(PACK):
+                transpose_own(2, b, t)
+                transpose_taken(2, b, t, taken_2[:, t, :])
         turn_back(2)
         finish(1)
-        sum_on_vector(3, nc.scalar.copy)
+
+        sum_on_vector(3, taken_3, nc.scalar.copy, planes_in_place_of="z_bf_0")
         finish(2)
         finish(3)
-        sum_on_vector(4, nc.vector.tensor_copy)
-        finish(4)
+        taken_last = tile("taken_last", [P, PACK * Z_PIECES[4][1]], F32, place_of="z_bf_1")
+        sum_on_vector(4, taken_last[:].rearrange("p (t c) -> p t c", t=PACK), nc.vector.tensor_copy)
+        finish(4, codes_in_place_of="z_bf_2")

from contextlib import ExitStack

import concourse.mybir as mybir
from concourse.masks import make_identity

K, T, S, H, N = 512, 2048, 1024, 512, 256
FLOPS = 2 * K * H * S + 2 * H * N * S

F32 = mybir.dt.float32
BF16 = mybir.dt.bfloat16
I32 = mybir.dt.int32
U32 = mybir.dt.uint32
U16 = mybir.dt.uint16
U8 = mybir.dt.uint8
FP8X4 = mybir.dt.float8_e4m3fn_x4
GELU = mybir.ActivationFunctionType.Gelu_apprx_tanh
MULT = mybir.AluOpType.mult
ADD = mybir.AluOpType.add

P = 128
PACK = 4
STRIPE = 16
BANK = 512
RUN = 4

X_LOADS = (
    ((1024, 1024), (512, 512), (512, 320)),
    ((512, 0), (512, 0), (512, 256), (256, 256), (256, 160)),
)

QUARTER = S // 4
QUARTERS = (0, 2, 3, 1)
WOVEN_ON_VECTOR = QUARTERS[:2]
WOVEN_ON_SCALAR = QUARTERS[2:]

Z_PIECES = ((0, 256), (256, 256), (512, 256), (768, 128), (896, 128))
LAST_ON_TENSOR = 2
LAST_PIECE = len(Z_PIECES) - 1

H_BANKS = (
    ((0, (0,)), (1, (2,)), (2, (3,)), (3, (1,))),
    ((0, (2, 3)), (1, (0, 1))),
    ((4, (0, 1)), (5, (2, 3))),
    ((6, (0, 1)), (7, (2, 3))),
)
SUM_BANKS = (2, 0, 4)
BACK_BANKS = (6, 7, 2)
OUT_BANKS = (3, 5, 0, 6, 3)


def tile_picked_treeup_gelu_e_kernel(tc, xT, w1, w2, share, offs, par, out):
    nc = tc.nc

    def entries(lst, first, count):
        return lst[:, first // STRIPE : (first + count) // STRIPE]

    def quantize(codes, scales, values):
        nc.vector.quantize_mx(out=codes.bitcast(FP8X4), scales=scales, in_=values)

    def product(acc, w_codes, w_scales, column, codes, scales):
        nc.tensor.matmul_mx(out=acc, lhsT=w_codes[:, column : column + P].bitcast(FP8X4),
                            lhsT_scale=w_scales[:, column : column + P],
                            rhs=codes[:].bitcast(FP8X4), rhs_scale=scales[:], start=True, stop=True)

    with ExitStack() as ctx:
        lists = ctx.enter_context(tc.tile_pool(name="lists", bufs=1))
        keep = ctx.enter_context(tc.tile_pool(name="keep", bufs=1))
        psum = ctx.enter_context(tc.psum_pool(name="psum", bufs=1))

        def tile(name, shape, dtype, place_of=None):
            return keep.tile(shape, dtype, name=name, tag=place_of or name, align_bytes=64)

        def bank(number):
            return psum.tile([P, BANK], F32, name="bank_%d" % number)

        offs_t = lists.tile([P, S // STRIPE], U16, name="offs_t")
        par_t = lists.tile([P, S // STRIPE], U16, name="par_t")

        zero = tile("zero", [P, 1], F32)
        no_bias = tile("no_bias", [P, 1], F32)
        nc.vector.memset(zero[:], 0.0)
        nc.scalar.activation(out=no_bias[:], in_=zero[:], func=GELU)

        ident = tile("ident", [P, P], F32)
        make_identity(nc, ident[:])

        x_rows = xT.rearrange("(p j) c -> p j c", j=PACK)
        x_raw = ([], [])
        for u in range(2):
            first = 0
            for cols, on_vector in X_LOADS[u]:
                raw = tile("x_raw_%d_%d" % (u, first), [P, 2, cols], F32)
                nc.sync.dma_start(out=raw[:], in_=x_rows[:, 2 * u : 2 * u + 2, first : first + cols])
                if (u, first) == (0, 0):
                    nc.sync.dma_start(offs_t[:], offs)
                x_raw[u].append((raw, first, cols, on_vector))
                first = first + cols
        w1_rows = w1.rearrange("(p j) c -> p j c", j=PACK)
        w1_raw = []
        for half in range(2):
            w1_raw.append(tile("w1_raw_%d" % half, [P, PACK, H // 2], F32))
            nc.sync.dma_start(out=w1_raw[half][:], in_=w1_rows[:, :, half * (H // 2) : (half + 1) * (H // 2)])
        head = Z_PIECES[0][1]
        share_head = tile("share_head", [P, head], F32)
        share_rest = tile("share_rest", [P, S - head], F32)
        nc.sync.dma_start(out=share_head[:], in_=share[:, 0:head])
        nc.sync.dma_start(out=share_rest[:], in_=share[:, head:S])
        nc.sync.dma_start(par_t[:], par)
        w2_raw = tile("w2_raw", [P, PACK, N], F32)
        nc.sync.dma_start(out=w2_raw[:], in_=w2.rearrange("(p j) c -> p j c", j=PACK))

        pairs = [tile("pairs_%d" % u, [P, T], U32) for u in range(2)]
        picked = {q: tile("picked_%d" % q, [P, 2 * QUARTER], U32) for q in QUARTERS}
        for u in range(2):
            halves = pairs[u][:].bitcast(BF16).rearrange("p (c e) -> p c e", e=2)
            for raw, first, cols, on_vector in x_raw[u]:
                rows = raw[:].rearrange("p e c -> p c e")
                if on_vector > 0:
                    nc.vector.tensor_copy(out=halves[:, first : first + on_vector, :], in_=rows[:, 0:on_vector, :])
                if on_vector < cols:
                    nc.scalar.copy(out=halves[:, first + on_vector : first + cols, :], in_=rows[:, on_vector:cols, :])
            for q in QUARTERS:
                nc.vector.tensor_copy(out=picked[q][:, u * QUARTER : (u + 1) * QUARTER],
                                      in_=pairs[u][:].indirect(entries(offs_t, q * QUARTER, QUARTER)))

        x_bf, x_codes, x_scales = {}, {}, {}

        def weave_x(q):
            word = I32 if q in WOVEN_ON_VECTOR else U32
            move = nc.vector.tensor_copy if q in WOVEN_ON_VECTOR else nc.scalar.copy
            move(out=x_bf[q].bitcast(word).rearrange("p (c u) -> p c u", u=2),
                 in_=picked[q][:].bitcast(word).rearrange("p (u c) -> p c u", u=2))

        def quantize_x(q):
            x_codes[q] = tile("x_codes_%d" % q, [P, QUARTER], U32)
            x_scales[q] = tile("x_scales_%d" % q, [P, QUARTER], U8)
            quantize(x_codes[q][:], x_scales[q][:], x_bf[q])

        for q in WOVEN_ON_VECTOR:
            x_bf[q] = tile("x_bf_%d" % q, [P, PACK * QUARTER], BF16)[:]
            weave_x(q)

        w1_bf = [tile("w1_bf_%d" % v, [P, 2, P, PACK], BF16) for v in range(2)]
        w1_codes, w1_scales = {}, {}

        def weave_w1(half, v):
            nc.scalar.copy(
                out=w1_bf[v][:, :, half * (P // 2) : (half + 1) * (P // 2), :].rearrange("p e m j -> p m j e"),
                in_=w1_raw[half][:].rearrange("p j (m t) -> p m j t", t=PACK)[:, :, :, 2 * v : 2 * v + 2])

        def quantize_w1(v):
            w1_codes[v] = tile("w1_codes_%d" % v, [P, 2 * P], U32)
            w1_scales[v] = tile("w1_scales_%d" % v, [P, 2 * P], U8)
            quantize(w1_codes[v][:], w1_scales[v][:], w1_bf[v][:].rearrange("p e m j -> p (e m j)"))

        weave_w1(0, 0)
        weave_w1(0, 1)
        weave_w1(1, 0)
        x_bf_late = tile("x_bf_late", [P, len(WOVEN_ON_SCALAR) * PACK * QUARTER], BF16, place_of="w1_raw_0")
        for nth, q in enumerate(WOVEN_ON_SCALAR):
            x_bf[q] = x_bf_late[:, PACK * QUARTER * nth : PACK * QUARTER * (nth + 1)]
            weave_x(q)
        weave_w1(1, 1)
        quantize_x(QUARTERS[0])
        quantize_w1(0)
        for q in QUARTERS[1:]:
            quantize_x(q)
        quantize_w1(1)

        w2_bf = tile("w2_bf", [P, N, PACK], BF16, place_of="w1_raw_0")
        nc.vector.tensor_copy(out=w2_bf[:].rearrange("p (c d) j -> p c j d", d=RUN),
                              in_=w2_raw[:].rearrange("p j (c d) -> p c j d", d=RUN))
        w2_codes = tile("w2_codes", [P, N], U32)
        w2_scales = tile("w2_scales", [P, N], U8)

        h = [tile("h_%d" % t, [P, S], F32) for t in range(PACK)]
        for t in range(PACK):
            for number, quarters in H_BANKS[t]:
                acc = bank(number)
                for nth, q in enumerate(quarters):
                    product(acc[:, nth * QUARTER : (nth + 1) * QUARTER], w1_codes[t // 2], w1_scales[t // 2],
                            (t % 2) * P, x_codes[q], x_scales[q])
                first, n = quarters[0] * QUARTER, len(quarters) * QUARTER
                nc.scalar.activation(out=h[t][:, first : first + n], in_=acc[:, 0:n], func=GELU, bias=no_bias[:])

        quantize(w2_codes[:], w2_scales[:], w2_bf[:].rearrange("p c j -> p (c j)"))

        out_rows = out.rearrange("(a p) c -> p a c", p=P)
        z_bf, sums = {}, {}

        def take(piece, t, taken):
            first, n = Z_PIECES[piece]
            factors = share_head[:] if piece == 0 else share_rest[:, first - head : first - head + n]
            nc.vector.tensor_tensor(out=taken, in0=h[t][:].indirect(entries(par_t, first, n)), in1=factors, op=MULT)

        def open_sums(piece):
            sums[piece] = [bank(SUM_BANKS[piece] + b) for b in range(Z_PIECES[piece][1] // P)]

        def transpose_own(piece, b, t):
            first = Z_PIECES[piece][0] + b * P
            nc.tensor.matmul(out=sums[piece][b][:, t * P : (t + 1) * P], lhsT=h[t][:, first : first + P],
                             rhs=ident[:], start=True, stop=False, is_transpose=True)

        def transpose_taken(piece, b, t, taken):
            nc.tensor.matmul(out=sums[piece][b][:, t * P : (t + 1) * P], lhsT=taken[:, b * P : (b + 1) * P],
                             rhs=ident[:], start=False, stop=True, is_transpose=True)

        def turn_back(piece):
            first, n = Z_PIECES[piece]
            batches = n // P
            z_rows = tile("z_rows_%d" % piece, [P, batches * H], BF16)
            z_bf[piece] = tile("z_bf_%d" % piece, [P, PACK * n], BF16)
            back = bank(BACK_BANKS[piece])
            for b in range(batches):
                row = z_rows[:, b * H : (b + 1) * H]
                nc.scalar.copy(out=row.rearrange("r (u p e) -> r u p e", u=2, e=2),
                               in_=sums[piece][b][:].rearrange("r (u e p) -> r u p e", u=2, e=2))
                for u in range(2):
                    column = (2 * b + u) * P
                    nc.tensor.transpose(back[:, column : column + P], row.bitcast(F32)[:, u * P : (u + 1) * P],
                                        ident[:])
            nc.scalar.copy(out=z_bf[piece][:].bitcast(F32).rearrange("p (b r u) -> p b r u", b=batches, u=2),
                           in_=back[:].rearrange("p (b u r) -> p b r u", b=batches, u=2))

        def sum_on_vector(piece, taken, weave, planes_in_place_of=None):
            first, n = Z_PIECES[piece]
            take(piece, 0, taken[:, 0, :])
            planes = tile("z_planes_%d" % piece, [P, PACK, n], BF16, place_of=planes_in_place_of)
            for t in range(PACK):
                if t + 1 < PACK:
                    take(piece, t + 1, taken[:, t + 1, :])
                nc.vector.tensor_tensor(out=planes[:, t, :], in0=taken[:, t, :], in1=h[t][:, first : first + n], op=ADD)
            z_bf[piece] = tile("z_bf_%d" % piece, [P, PACK * n], BF16)
            weave(out=z_bf[piece][:].rearrange("p (c d t) -> p c t d", d=RUN, t=PACK),
                  in_=planes[:].rearrange("p t (c d) -> p c t d", d=RUN))

        def finish(piece, codes_in_place_of=None):
            first, n = Z_PIECES[piece]
            codes = tile("z_codes_%d" % piece, [P, n], U32, place_of=codes_in_place_of)
            scales = tile("z_scales_%d" % piece, [P, n], U8)
            quantize(codes[:], scales[:], z_bf[piece][:])
            result = tile("result_%d" % piece, [P, N // P, n], F32)
            if piece in (LAST_ON_TENSOR, LAST_PIECE):
                for a, move in enumerate((nc.scalar.copy, nc.vector.tensor_copy)):
                    acc = bank(OUT_BANKS[piece] + a)
                    product(acc[:, 0:n], w2_codes, w2_scales, a * P, codes, scales)
                    move(out=result[:, a, :], in_=acc[:, 0:n])
            else:
                acc = bank(OUT_BANKS[piece])
                for a in range(N // P):
                    product(acc[:, a * n : (a + 1) * n], w2_codes, w2_scales, a * P, codes, scales)
                nc.scalar.copy(out=result[:].rearrange("p a c -> p (a c)"), in_=acc[:, 0 : (N // P) * n])
            nc.sync.dma_start(out=out_rows[:, :, first : first + n], in_=result[:])

        for t in range(PACK):
            for piece in range(2):
                if t == 0:
                    open_sums(piece)
                for b in range(len(sums[piece])):
                    transpose_own(piece, b, t)
                taken = tile("taken_%d_%d" % (piece, t), [P, Z_PIECES[piece][1]], F32)
                take(piece, t, taken[:])
                for b in range(len(sums[piece])):
                    transpose_taken(piece, b, t, taken)
        turn_back(0)
        turn_back(1)
        finish(0)

        wide, narrow = Z_PIECES[2][1], Z_PIECES[3][1]
        taken_middle = tile("taken_middle", [P, PACK * (wide + narrow)], F32, place_of="share_head")
        taken_2 = taken_middle[:, 0 : PACK * wide].rearrange("p (t c) -> p t c", t=PACK)
        taken_3 = taken_middle[:, PACK * wide : PACK * (wide + narrow)].rearrange("p (t c) -> p t c", t=PACK)
        for t in range(PACK):
            take(2, t, taken_2[:, t, :])
        open_sums(2)
        for b in range(len(sums[2])):
            for t in range(PACK):
                transpose_own(2, b, t)
                transpose_taken(2, b, t, taken_2[:, t, :])
        turn_back(2)
        finish(1)

        sum_on_vector(3, taken_3, nc.scalar.copy, planes_in_place_of="z_bf_0")
        finish(2)
        finish(3)
        taken_last = tile("taken_last", [P, PACK * Z_PIECES[4][1]], F32, place_of="z_bf_1")
        sum_on_vector(4, taken_last[:].rearrange("p (t c) -> p t c", t=PACK), nc.vector.tensor_copy)
        finish(4, codes_in_place_of="z_bf_2")
